import numpy as np, ml_dtypes
CORES = [40,41,42,43,44,45,46,47]
N = 8
BF = ml_dtypes.bfloat16
def gentries(a):
    return np.ascontiguousarray(a.reshape(8, 16, -1).transpose(0, 2, 1)).reshape(8, -1)
def gtable(e):
    e = np.asarray(e); return np.ascontiguousarray(e.reshape(8, -1, 16).transpose(0, 2, 1)).reshape(128, -1).astype(np.int32)
F, STEP, CAPP, V, R, D = 2048, 128, 80, 8192, 3, 2
def aim(rng, s):
    p = rng.integers(1, 64, F); o = rng.permutation(F); k = s - int(np.sum(p)); room = (63 - p if k > 0 else p - 1)[o]
    p[o] += np.sign(k) * np.clip(abs(k) - (np.add.accumulate(room) - room), 0, room)
    return p
def rise(rng):
    top = N * CAPP * STEP + int(rng.integers(62, STEP + 1)); lo, hi, best = F, N * CAPP * STEP, -1
    for k in range(20):
        s = (lo + hi) // 2 if k else F; v = aim(rng, s); z = v.copy()
        for a in range(R - 1):
            z[np.flatnonzero(np.diff(np.add.accumulate(z) // STEP, prepend=0))] = 63
        u = int(np.sum(z))
        if u >= top: hi = s
        else:
            lo = s
            if u > best: best, p, last = u, v, z
    total = np.concatenate([np.zeros(1, np.int64), np.add.accumulate(last)]) + 63 * (F - np.arange(F + 1))
    p[np.flatnonzero(total < top)[0]:] = 63
    return p
def links(rng):
    lab = rng.integers(0, rng.integers(8, 257), F); o = np.argsort(lab, kind="stable"); b, c = o[:-1], o[1:]
    on = (lab[b] == lab[c]) & (rng.random(F - 1) > 0.05); v = np.stack([np.arange(F), np.arange(F)])
    v[0, c[on]] = b[on]; v[1, b[on]] = c[on]
    return v
def whole(rng, m, *shape):
    return rng.integers(-m, m + 1, shape).astype(np.float32).astype(BF)
def draw(rng, lo, hi):
    v = np.stack([np.stack([links(rng) for g in range(8)]) for r in range(N)]).astype(np.int32)
    return {"x": whole(rng, 8, N, 128, F), "prv": np.ascontiguousarray(v[:, :, 0]), "nxt": np.ascontiguousarray(v[:, :, 1]), "key": rng.integers(0, V, (N, 8, F)).astype(np.int32), "rw": rng.integers(-255, 256, (N, 8, F)).astype(np.int32),
            "pri": np.stack([gtable(np.stack([aim(rng, int(rng.integers(lo * F, hi * F))) for g in range(8)])) for r in range(N)]), "w": whole(rng, 4, N, 128, 2 * D + 1), "val": whole(rng, 8, N, 128, V)}
def put(d, r, g, p):
    e = gentries(d["pri"][r]); e[g] = p; d["pri"][r] = gtable(e)
def setup_inputs(rng):
    return draw(rng, 24, 34)
def setup_inputs_full(rng):
    d = draw(rng, 24, 34); o = rng.permutation(N); late = rng.random((N, 8)) < 0.2; late[o[1], rng.permutation(8)[:4]] = True; late[o[0]] = False
    m = rng.random((N, 8)) < 0.3; m[o[0]] = True; m = m & ~late
    for r, g in np.argwhere(m):
        put(d, r, g, aim(rng, N * CAPP * STEP + int(rng.integers(0, STEP))))
        d["x"][r, 16 * g:16 * g + 16] = whole(rng, 1, 16, F); d["rw"][r, g] = rng.integers(-60, 61, F)
    for r, g in np.argwhere(late):
        put(d, r, g, rise(rng))
        d["x"][r, 16 * g:16 * g + 16] = 0; d["rw"][r, g] = 340; d["rw"][r, g, 0] = 0
    return d
def setup_inputs_even(rng):
    d = draw(rng, 24, 34)
    for r in range(N):
        d["pri"][r] = gtable(np.repeat(rng.permutation(np.array([16, 16, 16, 32, 32, 32, 32, 32]))[:, None], F, 1))
    return d
def setup_inputs_few(rng):
    d = draw(rng, 24, 34)
    for r in range(N):
        o = rng.permutation(8)[:4]
        for g in o[1:]: d["x"][r, 16 * g:16 * g + 16] = 0
        for g in o[:2]: put(d, r, g, np.ones(F, np.int64))
        for g in o[2:]: put(d, r, g, aim(rng, int(rng.integers(12 * F, 17 * F))))
        d["rw"][r, o[1]] = 0; d["rw"][r, o[2]] = rng.choice(np.array([0, 8, -8, 16, -16, 5, -5]), F); d["rw"][r, o[3]] = rng.choice(np.array([-336, -342, 336, 341, 335, 330]), F)
    return d
def setup_inputs_loose(rng):
    d = draw(rng, 8, 17); d["prv"] = rng.integers(0, F, (N, 8, F)).astype(np.int32); d["nxt"] = rng.integers(0, F, (N, 8, F)).astype(np.int32)
    for n, m in (("x", 8), ("w", 4), ("val", 8)):
        d[n] = (m * (2 * rng.integers(0, 2, d[n].shape) - 1)).astype(np.float32).astype(BF)
    d["rw"] = (1023 * rng.integers(-1, 2, (N, 8, F))).astype(np.int32)
    for r in range(N):
        o = rng.permutation(8)
        d["prv"][r, o[0]] = 0; d["nxt"][r, o[0]] = F - 1; d["prv"][r, o[1]] = np.arange(F); d["nxt"][r, o[1]] = np.arange(F)
        d["prv"][r, o[2]] = (np.arange(F) - 1) % F; d["nxt"][r, o[2]] = (np.arange(F) + 1) % F
        d["key"][r, o[3]] = V - 1; d["key"][r, o[4]] = rng.choice(np.array([0, V - 1]), F)
        d["x"][r, 16 * o[5]:16 * o[5] + 16] = 8
    q = rng.integers(0, N); d["w"][q] = 4; d["val"][q] = 8
    return d
def setup_inputs_spread(rng):
    d = draw(rng, 8, 17)
    for n, m in (("x", F), ("val", V)):
        s = np.left_shift(1, rng.integers(0, 4, (N, 1, m))) * (rng.random((N, 1, m)) > 0.0625)
        d[n] = (rng.integers(-1, 2, (N, 128, m)) * s).astype(np.float32).astype(BF)
    d["w"] = (rng.integers(-4, 5, (N, 128, 2 * D + 1)) * (rng.random((N, 128, 1)) > 0.4)).astype(np.float32).astype(BF)
    d["key"] = np.minimum(rng.random((N, 8, F)) ** 3 * V, V - 1).astype(np.int32)
    d["rw"] = np.right_shift(rng.integers(-1023, 1024, (N, 8, F)), rng.integers(0, 11, (N, 8, F))).astype(np.int32)
    return d
def play(x, prv, nxt, key, rw, pri, w, val):
    X = x.astype(np.float32).reshape(N, 8, 16, F); W = w.astype(np.float32).reshape(N, 8, 16, 2 * D + 1); A = val.astype(np.float32).reshape(N, 8, 16, V)
    P = np.stack([gentries(pri[r]) for r in range(N)]).astype(np.int64); most = 0
    for a in range(R):
        for r in range(N):
            for g in range(8):
                t = np.flatnonzero(np.diff(np.add.accumulate(P[r, g]) // STEP, prepend=0)); most = max(most, len(t))
                q = np.arange(len(t)) % N
                pt = {0: t}
                for k in range(1, D + 1):
                    pt[k] = nxt[r, g][pt[k - 1]]; pt[-k] = prv[r, g][pt[1 - k]]
                h = np.zeros((len(t), 16), np.float32)
                for k in range(-D, D + 1):
                    h += W[q, g, :, D + k] * X[r, g][:, pt[k]].T
                e = np.sum(A[q, g, :, key[r, g][t]] * h, axis=1) + (rw[r, g][pt[0]] + rw[r, g][pt[1]] + rw[r, g][pt[2]])
                P[r, g, t] = np.minimum(np.maximum(np.abs(e).astype(np.int64) >> 4, 1), 63)
    return P, most
def check_inputs(d):
    bad = []
    for n, lo, hi in (("x", -8, 8), ("prv", 0, F - 1), ("nxt", 0, F - 1), ("key", 0, V - 1), ("rw", -1023, 1023), ("pri", 1, 63), ("w", -4, 4), ("val", -8, 8)):
        v = np.asarray(d[n]).astype(np.float32)
        if not (np.isfinite(v).all() and (v == np.floor(v)).all() and v.min() >= lo and v.max() <= hi): bad.append(n)
    if not bad and play(**d)[1] > N * CAPP: bad.append("CAPP")
    return bad
def reference(x, prv, nxt, key, rw, pri, w, val):
    P, most = play(x, prv, nxt, key, rw, pri, w, val)
    y = np.stack([gtable(P[r]) for r in range(N)])
    return {"y": y.astype(np.float32)}

@@ -1,0 +1,397 @@
+import math
+from concourse.bass import DstId, RemoteDMATransfer
+from concourse.mybir import AluOpType, ActivationFunctionType
+
+N, F, V, R = 8, 2048, 8192, 3
+W = float(1 << 17)
+LN64 = math.log(64.0)
+OWN = 4
+RQ, VR = 128, 1920
+
+SBUF = {
+    "bfloat16": dict(xs=F, vs=V, ws=8, wex=2, um=128, lm=128, nl=128, idb=128, idk=128, em=240, gmb=8, pk=256, zb=128,
+                     dg=40 * 128, rtb=256, b0=F, b0p=F, a1=F, rwt=F, x1=F, x2=F, xm1=F, xm2=F, prb=128, gx=1024, pp=144,
+                     vr=VR * R, xg=6 * 1024, uu=128, zc=128, e1=128, sg=128, es=128, c1=128, c2=128, eb=256, ec=256),
+    "float32": dict(dif=128, c240=240, m16=128, j8=8, ktf=4, col=4, idf=128, gw=56, rst=128, npf=256, keyf=128, sm=128,
+                    z1=128, zz=128, cl=1024, ua=128, sa=128, sb=128, ea=256, ta=128, tb=128, yo=128),
+    "int32": dict(npi=256, keyi=128, rwi=128, prii=128, kci=4, a16=64, kti=4, npb=256, rti=256, si=128, low=128, t1=128,
+                  ki=64, ks=64, pl=64, kk=64, ri=128, pi=128),
+    "uint16": dict(npu=256, ppu=256, tu=64, tp=64, rq=RQ * R),
+    "float16": dict(gmh=8, prod=1024),
+}
+SCRATCH = {n: ("sbuf", [128, c], d) for d, group in SBUF.items() for n, c in group.items()}
+SCRATCH.update({n: ("psum", [128, 512], "float32") for n in ("qd", "qv", "qk", "qh0", "qh1", "qe", "qa", "qs")})
+SEMAPHORES = (["cv", "ca", "cp", "cg", "snd", "lw", "lpri", "lnx", "lpv", "lkey", "lrw", "lx", "lv0", "lv1", "lb0", "lb1", "sty"]
+              + ["wa%d" % h for h in range(2)]
+              + ["rq%d_%d" % (a, h) for a in range(R) for h in range(2)] + ["rt%d_%d" % (a, h) for a in range(R) for h in range(2)])
+
+A = AluOpType
+AF = ActivationFunctionType
+HALF = ((0, 1, 2, 3), (5, 6, 7))
+
+
+def asked(s):
+    return s if s < OWN else (N - 1 if s == OWN else s - 1)
+
+
+def kept(s):
+    return N - 1 + (s - OWN) % N
+
+
+def rank_program(g, core, T, topo):
+    rank = T.rank_of(core)
+    if rank is None:
+        return
+    Q = {"v": g.vector, "a": g.scalar, "p": g.tensor, "g": g, "s": g.sync}
+    CS = {"v": "cv", "a": "ca", "p": "cp", "g": "cg"}
+    count = {"v": 0, "a": 0, "p": 0, "g": 0}
+    known = {e: {} for e in Q}
+    wrote, read, bank = {}, {}, {}
+    totals = {}
+
+    def wait_for(e, events):
+        for sem, n, clock in sorted(events, key=lambda ev: -ev[1]):
+            if known[e].get(sem, 0) < n:
+                Q[e].wait_ge(T.sem[sem], n)
+                known[e][sem] = n
+                for k, m in clock.items():
+                    known[e][k] = max(known[e].get(k, 0), m)
+
+    def before(e, rd, wr, ps):
+        ev = [wrote[r] for r in rd if r in wrote]
+        for w in wr:
+            ev += read.get(w, []) + ([wrote[w]] if w in wrote else [])
+        for b in ps:
+            ev += [x for q, x in bank.get(b, {}).items() if q != e]
+        if e == "p":
+            ev = [x for x in ev if x[0] != "cp"]
+        wait_for(e, ev)
+
+    def after(e, ev, rd, wr, ps):
+        for r in rd:
+            read.setdefault(r, []).append(ev)
+        for w in wr:
+            wrote[w] = ev
+            read[w] = []
+        for b in ps:
+            bank.setdefault(b, {})[e] = ev
+        totals[ev[0]] = max(totals.get(ev[0], 0), ev[1])
+
+    def op(e, make, rd, wr, ps=()):
+        before(e, rd, wr, ps)
+        count[e] += 1
+        make().then_inc(T.sem[CS[e]], 1)
+        after(e, (CS[e], count[e], dict(known[e])), rd, wr, ps)
+
+    def dma(e, sem, out, in_, rd, wr):
+        before(e, rd, wr, ())
+        Q[e].dma_start(out, in_).then_inc(T.sem[sem], 16)
+        after(e, (sem, 16, dict(known[e])), rd, wr, ())
+
+    v, act, pe = g.vector, g.scalar, g.tensor
+
+    def ts(out, in0, s1, op0, s2, op1, rd, wr, ps=()):
+        if op1 is None:
+            op("v", lambda: v.tensor_scalar(out, in0, s1, None, op0), rd, wr, ps)
+        else:
+            op("v", lambda: v.tensor_scalar(out, in0, s1, s2, op0, op1), rd, wr, ps)
+
+    def tt(out, in0, in1, o, rd, wr, ps=()):
+        op("v", lambda: v.tensor_tensor(out, in0, in1, o), rd, wr, ps)
+
+    def cp(out, in_, rd, wr, ps=()):
+        op("v", lambda: v.tensor_copy(out, in_), rd, wr, ps)
+
+    def ms(ap, c, wr):
+        op("v", lambda: v.memset(ap, c), (), wr)
+
+    def ac(out, in_, func, bias, scale, rd, wr, ps=()):
+        op("a", lambda: act.activation(out, in_, func, bias=bias, scale=scale), rd, wr, ps)
+
+    def mm(out, lhsT, rhs, start, stop, rd, wr, ps):
+        op("p", lambda: pe.matmul(out, lhsT, rhs, start, stop), rd, wr, ps)
+
+    def gather(e, out, win, off, rd, wr):
+        if e == "v":
+            cp(out, win.indirect(off), rd, wr)
+        else:
+            ac(out, win.indirect(off), AF.Identity, 0.0, 1.0, rd, wr)
+
+    sent = [0]
+
+    def send(sem, h, step, src, dst, rd, wr):
+        before("g", rd, (), ())
+        tr = []
+        for j, s in enumerate(HALF[h]):
+            to = T.cores[(rank + step * (s + 4)) % N]
+            rid, pid, _ = topo.addr(to)
+            mask = sum(1 << e for e in topo.engines(core, to)[j::4])
+            tr.append(RemoteDMATransfer(dst_ids=[DstId(rid=rid, pnc=pid)], dma_engine_mask=mask,
+                                        remote_sem=T.sem[sem], src=src(s), dst=dst(s)))
+        g.remote_dma_fused(tr, local_sem=T.sem.snd)
+        sent[0] += 4 * len(tr)
+        wrote[wr] = (sem, 4 * len(tr), {})
+        totals[sem] = 4 * len(tr)
+
+    dma("s", "lnx", T.npi[:, 0:128], T.nxt[:], (), ["nxi"])
+    dma("s", "lpri", T.prii[:], T.pri[:], (), ["prii"])
+    dma("s", "lx", T.xs[:], T.x[:], (), ["xs"])
+    dma("s", "lkey", T.keyi[:], T.key[:], (), ["keyi"])
+    dma("s", "lw", T.ws[:, 0:5], T.w[:], (), ["ws"])
+    dma("s", "lrw", T.rwi[:], T.rw[:], (), ["rwi"])
+    dma("s", "lpv", T.npi[:, 128:256], T.prv[:], (), ["pvi"])
+    dma("s", "lv0", T.vs[:, 0:V // 2], T.val[:, 0:V // 2], (), ["vs0"])
+
+    def iota(out, pattern, base, cm, wr, fl=True):
+        if fl:
+            op("g", lambda: g.iota(out, pattern, base, cm, allow_small_or_imprecise_dtypes=True), (), wr)
+        else:
+            op("g", lambda: g.iota(out, pattern, base, cm), (), wr)
+    iota(T.kci[:, 0:1], [[1, 1]], 0, 1, ["kc0"], False)
+    iota(T.j8[:], [[1, 8]], 0, 0, ["j8"])
+    iota(T.dif[:], [[1, 128]], 0, -1, ["dif"])
+    iota(T.c240[:], [[1, 240]], -112, 0, ["c240"])
+    iota(T.m16[:], [[1, 8], [0, 16]], 0, 0, ["m16"])
+    iota(T.a16[:], [[0, 8], [16, 8]], 0, 0, ["a16"], False)
+    iota(T.b0[:], [[0, F]], 0, 0, ["b0h", "b0l"])
+
+    ms(T.rst[:], 1.0, ["rst"])
+    ms(T.gw[:], 0.0, ["gmf", "gmn"])
+    ms(T.zb[:], 0.0, ["zb"])
+    ms(T.pp[:, 0:16], 0.0, ["pp0"])
+    ts(T.kti[:, 0:1], T.kci[:, 0:1], 15, A.bitwise_and, None, None, ["kc0"], ["kt0"])
+    ts(T.kti[:, 1:2], T.kci[:, 0:1], 4, A.arith_shift_right, None, None, ["kc0"], ["kt1"])
+    ts(T.kti[:, 2:3], T.kci[:, 0:1], 7, A.bitwise_and, None, None, ["kc0"], ["kt2"])
+    ts(T.kti[:, 3:4], T.kci[:, 0:1], 3, A.arith_shift_right, 3, A.bitwise_and, ["kc0"], ["kt3"])
+    ms(T.rst[:, 0:128:16], 0.0, ["rst"])
+    cp(T.ktf[:], T.kti[:], ["kt0", "kt1", "kt2", "kt3"], ["ktf"])
+    kmod, kdiv, k7, k3 = T.ktf[:, 0:1], T.ktf[:, 1:2], T.ktf[:, 2:3], T.ktf[:, 3:4]
+    gmf = T.gw[:, 24:32]
+    ts(T.um[:], T.dif[:], 0.0, A.is_ge, None, None, ["dif"], ["um"])
+    ts(gmf, T.j8[:], kdiv, A.is_equal, None, None, ["j8", "ktf"], ["gmf"])
+    ts(T.gw[:, 16:24], T.j8[:], kdiv, A.is_equal, -1.0, A.mult, ["j8", "ktf"], ["gmn"])
+    ts(T.col[:, 0:1], kmod, -4.0 * W, A.add, None, None, ["ktf"], ["col0"])
+    ts(T.col[:, 1:2], kmod, 128.0, A.mult, None, None, ["ktf"], ["col1"])
+    ts(T.lm[:], T.dif[:], 0.0, A.is_lt, None, None, ["dif"], ["lm"])
+    ts(T.idf[:], T.dif[:], 0.0, A.is_equal, None, None, ["dif"], ["idf"])
+    ts(T.em[:], T.c240[:], kmod, A.is_equal, None, None, ["c240", "ktf"], ["em"])
+    ts(T.nl[:], T.dif[:], 0.0, A.is_lt, -1.0, A.mult, ["dif"], ["nl"])
+    ts(T.idk[:], T.dif[:], 0.0, A.is_equal, 1024.0, A.mult, ["dif"], ["idk"])
+    ac(T.wex[:, 0:1], k3, AF.Exp, 3.0 * LN64, -LN64, ["ktf"], ["wex0"])
+    ac(T.wex[:, 1:2], k3, AF.Exp, 0.0, LN64, ["ktf"], ["wex1"])
+    ac(T.col[:, 2:4], T.wex[:], AF.Identity, 0.0, 1.0, ["wex0", "wex1"], ["col2"])
+    ac(T.idb[:], T.idf[:], AF.Identity, 0.0, 1.0, ["idf"], ["idb"])
+    ac(T.gmb[:], gmf, AF.Identity, 0.0, 1.0, ["gmf"], ["gmb"])
+
+    P = T.pp[:, 16:144]
+    cp(T.npu[:, 0:128], T.npi[:, 0:128], ["nxi"], ["nxu"])
+    cp(T.prb[:], T.prii[:], ["prii"], ["prb"])
+    cp(T.gmh[:], gmf, ["gmf"], ["gmh"])
+    for j in range(8):
+        ts(T.gx[:, 128 * j:128 * j + 128], T.prb[:], T.gw[:, 24 + j:25 + j], A.mult, None, None, ["prb", "gmf"], ["gx%d" % j])
+    for j in range(8):
+        mm(T.qs[:, 0:128], T.em[:, 112 - 16 * j:240 - 16 * j], T.gx[:, j:1024:8], j == 0, j == 7,
+           ["em"] + ["gx%d" % k for k in range(8)], ["qs0"], ["qs"])
+    gather("a", T.x1[:], T.xs[:, 0:F], T.npu[:, 0:128], ["xs", "nxu"], ["x1"])
+    for k in range(2):
+        ts(T.pk[:, 128 * k:128 * k + 128], T.m16[:], k7, A.is_equal, T.col[:, 2 + k:3 + k], A.mult, ["m16", "ktf", "col2"], ["pk%d" % k])
+    cp(T.keyf[:], T.keyi[:], ["keyi"], ["keyf"])
+    op("p", lambda: pe.transpose(T.qk[:, 0:128], T.keyf[:], T.idf[:]), ["keyf", "idf"], ["qk1"], ["qk"])
+    cp(P, T.qs[:, 0:128], ["qs0"], ["pp"], ["qs"])
+    for d in range(5):
+        ts(T.dg[:, 128 * (5 * OWN + d):128 * (5 * OWN + d) + 128], T.idb[:], T.ws[:, d:d + 1], A.mult, None, None,
+           ["idb", "ws"], ["dgo%d" % d])
+    ts(T.qv[:, 0:128], T.qk[:, 0:128], 16.0, A.mult, T.col[:, 0:1], A.add, ["qk1", "col0"], ["base"], ["qk", "qv"])
+    ts(T.rti[:, 0:128], T.rwi[:], 5, A.arith_shift_right, None, None, ["rwi"], ["rt0"])
+    ts(T.rti[:, 128:256], T.rwi[:], 31, A.bitwise_and, None, None, ["rwi"], ["rt1"])
+    cp(T.npu[:, 128:256], T.npi[:, 128:256], ["pvi"], ["pvu"])
+    ts(T.rtb[:, 0:128], T.rti[:, 0:128], 32.0, A.mult, None, None, ["rt0"], ["rb0"])
+    cp(T.rtb[:, 128:256], T.rti[:, 128:256], ["rt1"], ["rb1"])
+    gather("a", T.xm1[:], T.xs[:, 0:F], T.npu[:, 128:256], ["xs", "pvu"], ["xm1"])
+    dma("s", "lb0", T.b0[0:128:16, :], T.rtb[:, 0:128], ["rb0"], ["b0h"])
+    dma("s", "lb1", T.b0[1:128:16, :], T.rtb[:, 128:256], ["rb1"], ["b0l"])
+    dma("s", "lv1", T.vs[:, V // 2:V], T.val[:, V // 2:V], (), ["vs1"])
+
+    samp, tv, cst = T.qv[:, 128:256], T.qv[:, 256:384], T.qv[:, 384:512]
+    QK = [(T.qd, 256, "qd"), (T.qk, 0, "qk")]
+    QH = [(T.qh0, "qh0"), (T.qh1, "qh1")]
+    QE = [(T.qe, "qe"), (T.qs, "qs")]
+
+    def forward(a, relus):
+        mm(T.qd[:, 128:256], T.idk[:], P, True, True, ["idk", "pp"], ["p1k"], ["qd"])
+        mm(T.qd[:, 0:128], T.um[:], P, True, False, ["um", "pp"], ["dd"], ["qd"])
+        mm(T.qd[:, 0:128], T.lm[:], T.pp[:, 15:143], False, False, ["lm", "pp", "pp0"], ["dd"], ["qd"])
+        mm(T.qd[:, 16:128:16], T.nl[:], T.pp[:, 31:143:16], False, True, ["nl", "pp"], ["dd"], ["qd"])
+        op("v", lambda: v.tensor_tensor_scan(T.sm[:], T.rst[:], T.qd[:, 0:128], 0.0, A.mult, A.add), ["rst", "dd"], ["sm"], ["qd"])
+        ts(T.si[:], T.sm[:], 1024.0, A.mult, (-rank - 5) % N * W, A.add, ["sm"], ["si"])
+        ts(T.low[:], T.si[:], 127 << 10, A.bitwise_and, None, None, ["si"], ["low"])
+        ts(T.t1[:], T.si[:], 7 << 17, A.bitwise_and, None, None, ["si"], ["t1"])
+        tt(samp, T.low[:], T.qd[:, 128:256], A.is_lt, ["low", "p1k"], ["samp"], ["qd", "qv"])
+        tt(T.z1[:], T.t1[:], T.qv[:, 0:128], A.add, ["t1", "base"], ["z1"], ["qv"])
+        tt(T.zz[:], T.z1[:], samp, A.mult, ["z1", "samp"], ["zz"], ["qv"])
+        for s in range(N):
+            lo, out = (s - 4) * W, T.cl[:, 128 * s:128 * s + 128]
+            if s < 4:
+                ts(out, T.zz[:], lo, A.max, lo + W, A.min, ["zz"], ["cl%d" % s])
+                mm(T.qd[:, 256 + 8 * s:264 + 8 * s], out, gmf, True, True, ["cl%d" % s, "gmf"], ["qk0"], ["qd"])
+                continue
+            if relus == "a":
+                ac(out, T.zz[:], AF.Relu, -lo, 1.0, ["zz"], ["cl%d" % s])
+            else:
+                ts(out, T.zz[:], -lo, A.add, 0.0, A.max, ["zz"], ["cl%d" % s])
+            mm(T.qk[:, 0:32], out, T.gw[:, 56 - 8 * s:88 - 8 * s], s == 4, s == 7, ["cl%d" % s, "gmf", "gmn"], ["qk1"], ["qk"])
+
+        def ask(h, between):
+            buf, c0, b = QK[h]
+            c = slice(32 * h, 32 * h + 32)
+            cp(T.ki[:, c], buf[:, c0:c0 + 32], ["qk%d" % h], ["ki%d" % h], [b])
+            ts(T.ks[:, c], T.ki[:, c], 4, A.arith_shift_right, V - 1, A.bitwise_and, ["ki%d" % h], ["ks%d" % h])
+            between()
+            k0 = RQ * a + 8 * kept(4 * h)
+            cp(T.rq[:, k0:k0 + 32], T.ks[:, c], ["ks%d" % h], ["ku%d_%d" % (a, h)])
+            send("rq%d_%d" % (a, h), h, 1, lambda s: T.rq[:, RQ * a + 8 * kept(s):RQ * a + 8 * kept(s) + 8],
+                 lambda s: T.rq[:, RQ * a + 8 * asked(s):RQ * a + 8 * asked(s) + 8], ["ku%d_%d" % (a, h)], "req%d_%d" % (a, h))
+        ts(T.uu[:], T.t1[:], 1.0 / W, A.mult, -3.5, A.add, ["t1"], ["uu"])
+        ask(0, lambda: tt(T.zc[:], T.uu[:], samp, A.mult, ["uu", "samp"], ["zc"], ["qv"]))
+        ask(1, lambda: ts(T.pl[:], T.ki[:], 15, A.bitwise_and, None, None, ["ki0", "ki1"], ["pl"]))
+        tt(T.kk[:], T.pl[:], T.a16[:], A.add, ["pl", "a16"], ["kk"])
+        ts(T.tp[:], T.kk[:], 16.0, A.mult, kmod, A.add, ["kk", "ktf"], ["tp"])
+        ts(T.tu[:], T.kk[:], T.col[:, 1:2], A.add, None, None, ["kk", "col1"], ["tu"])
+
+    def scales_1():
+        ac(T.c1[:], P, AF.Identity, 32.0, -1.0, ["pp"], ["c1"])
+        ac(T.ua[:], T.zc[:], AF.Abs, 0.0, 1.0, ["zc"], ["ua"])
+        ac(T.sg[:], T.zc[:], AF.Sign, 0.0, 1.0, ["zc"], ["sg"])
+        ac(T.e1[:], T.ua[:], AF.Exp, 0.5 * LN64, -LN64, ["ua"], ["e1"])
+
+    def scales_2():
+        tt(T.c2[:], T.c1[:], samp, A.mult, ["c1", "samp"], ["c2"], ["qv"])
+        tt(T.es[:], T.e1[:], T.sg[:], A.mult, ["e1", "sg"], ["es"])
+        tt(cst, T.c2[:], P, A.add, ["c2", "pp"], ["cst"], ["qv"])
+
+    def scales_3():
+        ac(T.sa[:], T.es[:], AF.Relu, 0.0, -1.0, ["es"], ["sa"])
+        ac(T.sb[:], T.es[:], AF.Relu, 0.0, 1.0, ["es"], ["sb"])
+
+    TAB = {0: (T.xm2, "xm2"), 1: (T.xm1, "xm1"), 2: (T.xs, "xs"), 3: (T.x1, "x1"), 4: (T.x2, "x2"), 5: (T.rwt, "rwt")}
+
+    def pick(e, d, h, last=False):
+        tab, name = TAB[d]
+        off, on = (T.tu, "tu") if d == 2 else (T.tp, "tp")
+        c0 = 1024 * d + 512 * h
+        gather(e, T.xg[:, c0:c0 + 512], tab[:, 0:F], off[:, 32 * h:32 * h + 32], [name, on], ["g%d_%d" % (d, h)])
+        if d == 5:
+            for i in range(16):
+                mm(QE[h][0][0:32, i:128:16], T.xg[:, c0 + i:c0 + 512:16], T.gmb[:], False, False,
+                   ["g5_%d" % h, "gmb"], ["qe%d" % h], [QE[h][1]])
+            return
+        for k in range(4):
+            s = 4 * h + k
+            mm(QH[h][0][:, 128 * k:128 * k + 128], T.dg[:, 128 * (5 * s + d):128 * (5 * s + d) + 128],
+               T.xg[:, c0 + 128 * k:c0 + 128 * k + 128], False, last and k == 3,
+               ["dg%d" % h, "dgo%d" % d, "g%d_%d" % (d, h)], ["qh%d" % h], [QH[h][1]])
+
+    def serve(a, e, h):
+        c0 = VR * a + 512 * h
+        gather(e, T.vr[:, c0:c0 + 512], T.vs[:, 0:V], T.rq[:, RQ * a + 32 * h:RQ * a + 32 * h + 32],
+               ["vs0", "vs1", "req%d_%d" % (a, h)] + ["ku%d_1" % a] * h, ["vg%d_%d" % (a, h)])
+        send("rt%d_%d" % (a, h), h, -1, lambda s: T.vr[:, VR * a + 128 * asked(s):VR * a + 128 * asked(s) + 128],
+             lambda s: T.vr[:, VR * a + 128 * kept(s):VR * a + 128 * kept(s) + 128], ["vg%d_%d" % (a, h)], "ret%d_%d" % (a, h))
+
+    def open_sums():
+        for h in range(2):
+            mm(QH[h][0][:], T.zb[:], T.xs[:, 0:512], True, False, ["zb", "xs"], ["qh%d" % h], [QH[h][1]])
+            mm(QE[h][0][0:32, 0:128], T.zb[:, 0:32], T.zb[:], True, False, ["zb"], ["qe%d" % h, "qs0"], [QE[h][1]])
+
+    def errors(a, h):
+        r0 = VR * a + 128 * kept(4 * h)
+        for c in range(2):
+            c0 = 512 * h + 256 * c
+            tt(T.prod[:, c0:c0 + 256], QH[h][0][:, c:512:2], T.vr[:, r0 + c:r0 + 512:2], A.mult,
+               ["qh%d" % h, "ret%d_%d" % (a, h)] + ["vg%d_1" % a] * h, ["pr%d_%d" % (h, c)], [QH[h][1]])
+            for i in range(c, 16, 2):
+                mm(QE[h][0][0:32, i:128:16], T.prod[:, c0 + i // 2:c0 + 256:8], T.gmh[:], False, i == 15,
+                   ["pr%d_%d" % (h, c), "gmh"], ["qe%d" % h], [QE[h][1]])
+
+    def sizes(h):
+        ac(T.ea[0:32, 128 * h:128 * h + 128], QE[h][0][0:32, 0:128], AF.Abs, 0.0, 0.0625, ["qe%d" % h], ["ea%d" % h], [QE[h][1]])
+
+    def digits(h):
+        c = slice(128 * h, 128 * h + 128)
+        ts(T.eb[0:32, c], T.ea[0:32, c], 127.53125, A.add, 191.0, A.min, ["ea%d" % h], ["eb%d" % h])
+        ts(T.ec[0:32, c], T.eb[0:32, c], 129.0, A.max, -160.0, A.add, ["eb%d" % h], ["ec%d" % h])
+        mm(T.qa[:, c], T.pk[0:32, c], T.ec[0:32, c], True, True, ["pk%d" % h, "ec%d" % h], ["qa%d" % h], ["qa"])
+
+    def finish(a):
+        sizes(0)
+        digits(0)
+        errors(a, 1)
+        tt(T.ta[:], T.qa[:, 0:128], T.sa[:], A.mult, ["qa0", "sa"], ["ta"], ["qa"])
+        sizes(1)
+        tt(tv, T.ta[:], cst, A.add, ["ta", "cst"], ["tv"], ["qv"])
+        digits(1)
+        tt(T.tb[:], T.qa[:, 128:256], T.sb[:], A.mult, ["qa1", "sb"], ["tb"], ["qa"])
+        tt(T.ri[:], T.tb[:], tv, A.add, ["tb", "tv"], ["ri"], ["qv"])
+        ts(T.pi[:], T.ri[:], 63, A.bitwise_and, None, None, ["ri"], ["pi"])
+        cp(P, T.pi[:], ["pi"], ["pp"])
+
+    forward(0, "v")
+    for h in range(2):
+        send("wa%d" % h, h, -1, lambda s: T.dg[:, 640 * OWN:640 * OWN + 640], lambda s: T.dg[:, 640 * s:640 * s + 640],
+             ["dgo%d" % d for d in range(5)], "dg%d" % h)
+    ts(T.npb[:], T.npi[:], 7, A.arith_shift_right, None, None, ["nxi", "pvi"], ["npb"])
+    ts(T.qa[:, 256:512], T.npb[:], -2047.0 / 16.0, A.mult, None, None, ["npb"], ["qa2"], ["qa"])
+    tt(T.npf[:], T.npi[:], T.qa[:, 256:512], A.add, ["nxi", "pvi", "qa2"], ["npf"], ["qa"])
+    ts(T.ppu[:], T.npf[:], 16.0, A.mult, None, None, ["npf"], ["ppu"])
+    open_sums()
+    scales_1()
+    gather("a", T.x2[:], T.x1[:, 0:F], T.ppu[:, 0:128], ["x1", "ppu"], ["x2"])
+    for i in range(16):
+        cp(T.b0p[:, i:F:16], T.b0[:, 128 * i:128 * i + 128], ["b0h", "b0l"], ["b0p%d" % i])
+    b0p = ["b0p%d" % i for i in range(16)]
+    tt(T.a1[:], T.b0[:, 0:F].indirect(T.npu[:, 0:128]), T.b0p[:], A.add, ["b0h", "b0l", "nxu"] + b0p, ["a1"])
+    scales_2()
+    gather("a", T.xm2[:], T.xm1[:, 0:F], T.ppu[:, 128:256], ["xm1", "ppu"], ["xm2"])
+    serve(0, "v", 0)
+    serve(0, "v", 1)
+    tt(T.rwt[:], T.a1[:, 0:F].indirect(T.ppu[:, 0:128]), T.b0p[:], A.add, ["a1", "ppu"] + b0p, ["rwt"])
+    scales_3()
+    pick("a", 2, 0), pick("a", 3, 0), pick("a", 1, 0), pick("a", 4, 0)
+    pick("v", 5, 0), pick("a", 0, 0, True)
+    pick("v", 5, 1), pick("a", 2, 1)
+    errors(0, 0)
+    pick("a", 3, 1), pick("v", 1, 1), pick("a", 4, 1), pick("v", 0, 1, True)
+    finish(0)
+
+    for a in range(1, R):
+        forward(a, "a")
+        open_sums()
+        scales_1()
+        pick("a", 3, 0)
+        scales_2()
+        pick("v", 5, 0)
+        scales_3()
+        pick("a", 2, 0), pick("v", 1, 0)
+        serve(a, "a", 0)
+        serve(a, "v", 1)
+        pick("a", 4, 0), pick("v", 0, 0, True)
+        pick("a", 2, 1), pick("v", 5, 1), pick("a", 3, 1), pick("v", 1, 1)
+        errors(a, 0)
+        pick("a", 4, 1), pick("a", 0, 1, True)
+        finish(a)
+
+    for j in range(8):
+        if j < 5:
+            ts(T.gx[:, j:1024:8], P, T.gw[:, 24 + j:25 + j], A.mult, None, None, ["pp", "gmf"], ["sx%d" % j])
+        else:
+            ac(T.gx[:, j:1024:8], P, AF.Identity, 0.0, T.gw[:, 24 + j:25 + j], ["pp", "gmf"], ["sx%d" % j])
+    for j in range(8):
+        mm(T.qk[:, 0:128], T.em[:, 112 - 16 * j:240 - 16 * j], T.gx[:, 128 * j:128 * j + 128], j == 0, j == 7,
+           ["em"] + ["sx%d" % k for k in range(8)], ["qk1"], ["qk"])
+    cp(T.yo[:], T.qk[:, 0:128], ["qk1"], ["yo"], ["qk"])
+    dma("s", "sty", T.y[:], T.yo[:], ["yo"], ["y"])
+    g.wait_ge(T.sem.snd, sent[0])
+    for sem, n in totals.items():
+        if sem != "sty" and max(k.get(sem, 0) for k in known.values()) < n:
+            g.wait_ge(T.sem[sem], n)
+    g.sync.wait_ge(T.sem.sty, 16)

@@ -3,31 +3,34 @@ from concourse.bass import DstId, RemoteDMATransfer
 from concourse.mybir import AluOpType, ActivationFunctionType
 
 N, F, V, R = 8, 2048, 8192, 3
-W = float(1 << 17)
+W = 1 << 20
 LN64 = math.log(64.0)
 OWN = 4
 RQ, VR = 128, 1920
+ND = 5
+START, ASTART, WAKE, GATHER, LOAD, ISSUE, FLIGHT, FIRST = 60, 100, 60, 1.56, 1300, 750, 1800, 3500
 
 SBUF = {
-    "bfloat16": dict(xs=F, vs=V, ws=8, wex=2, um=128, lm=128, nl=128, idb=128, idk=128, em=240, gmb=8, pk=256, zb=128,
-                     dg=40 * 128, rtb=256, b0=F, b0p=F, a1=F, rwt=F, x1=F, x2=F, xm1=F, xm2=F, prb=128, gx=1024, pp=144,
-                     vr=VR * R, xg=6 * 1024, uu=128, zc=128, e1=128, sg=128, es=128, c1=128, c2=128, eb=256, ec=256),
-    "float32": dict(dif=128, c240=240, m16=128, j8=8, ktf=4, col=4, idf=128, gw=56, rst=128, npf=256, keyf=128, sm=128,
-                    z1=128, zz=128, cl=1024, ua=128, sa=128, sb=128, ea=256, ta=128, tb=128, yo=128),
-    "int32": dict(npi=256, keyi=128, rwi=128, prii=128, kci=4, a16=64, kti=4, npb=256, rti=256, si=128, low=128, t1=128,
-                  ki=64, ks=64, pl=64, kk=64, ri=128, pi=128),
+    "bfloat16": dict(xs=F, vs=V, ws=8, turn=8, wex=2, um=128, lm=128, nl=128, idb=128, i32=128, nid=128,
+                     em=240, pk=128, zb=128, ma=128, mb=128, c240=240, dif=128, m16=128, g1=32,
+                     dg=N * ND * 128, x1=F, x2=F, xm1=F, xm2=F, b0=F, b1=F, r1=F, r3=F, rtb=256, prb=128,
+                     gx=1024, pp=144, vr=VR * R, xg=6 * 1024, uu=128, samp=128, dp=128, sab=256, eb=256, ec=256),
+    "float32": dict(ktf=6, j8=8, col=8, idf=128, gw=56, rst=128, keyf=128, sm=128, zz=128, cl=1024, ea=256, yo=128, npf=256),
+    "int32": dict(npi=256, npb=256, keyi=128, rwi=128, prii=128, kci=2, kti=6, rti=256, si=128, low=128, t1=128,
+                  ki=64, ks=64, pl=64, ta=128, tb=128, ri=128, pi=128),
     "uint16": dict(npu=256, ppu=256, tu=64, tp=64, rq=RQ * R),
-    "float16": dict(gmh=8, prod=1024),
+    "float16": dict(prod=1024),
 }
 SCRATCH = {n: ("sbuf", [128, c], d) for d, group in SBUF.items() for n, c in group.items()}
-SCRATCH.update({n: ("psum", [128, 512], "float32") for n in ("qd", "qv", "qk", "qh0", "qh1", "qe", "qa", "qs")})
-SEMAPHORES = (["cv", "ca", "cp", "cg", "snd", "lw", "lpri", "lnx", "lpv", "lkey", "lrw", "lx", "lv0", "lv1", "lb0", "lb1", "sty"]
+SCRATCH.update({n: ("psum", [128, 512], "float32") for n in ("qd", "qv", "qk", "qa", "qh0", "qh1", "qe0", "qe1")})
+SEMAPHORES = (["cv", "ca", "cp", "cg", "snd", "lw", "lpri", "lnx", "lpv", "lkey", "lrw", "lx", "lv0", "lv1", "lb0", "lb1", "lb2", "lb3", "sty"]
               + ["wa%d" % h for h in range(2)]
               + ["rq%d_%d" % (a, h) for a in range(R) for h in range(2)] + ["rt%d_%d" % (a, h) for a in range(R) for h in range(2)])
 
 A = AluOpType
 AF = ActivationFunctionType
 HALF = ((0, 1, 2, 3), (5, 6, 7))
+ORDER = ((3, 2, 1, 0), (4, 5, 6, 7))
 
 
 def asked(s):
@@ -35,362 +38,394 @@ def asked(s):
 
 
 def kept(s):
-    return N - 1 + (s - OWN) % N
+    return N - 1 + (s - OWN if s >= OWN else N - 1 - s)
+
+
+DEALT = []
+
+
+def deal(calls):
+    wrote, read = {}, {}
+    for k, c in enumerate(calls):
+        pre = {wrote[r] for r in c["rd"] + c["wr"] if r in wrote}
+        for w in c["wr"]:
+            pre.update(read.get(w, ()))
+        c["pre"] = pre - {k}
+        for r in c["rd"]:
+            read.setdefault(r, []).append(k)
+        for w in c["wr"]:
+            wrote[w], read[w] = k, []
+    if not DEALT:
+        taken, last = {}, {}
+        for c in calls:
+            e = c["e"]
+            t = max([0 if e == "p" else last.get(e, 0)] + [calls[j]["end"] + (0 if calls[j]["e"] == e else WAKE) for j in c["pre"]])
+            spans = [x for x in taken.get(e, []) if x[1] > t]
+            spans += [(a - WAKE, b + WAKE, q) for bk in c["ps"] for a, b, q in taken.get(bk, []) if q != e and b + WAKE > t]
+            for a, b, _ in sorted(spans):
+                if a >= t + c["busy"]:
+                    break
+                t = max(t, b)
+            c["start"], c["end"], last[e] = t, t + c["busy"] + c["way"], t + c["busy"]
+            for r in (e,) + tuple(c["ps"]):
+                taken.setdefault(r, []).append((t, t + c["busy"], e))
+        DEALT.extend(sorted(range(len(calls)), key=lambda k: (calls[k]["start"], k)))
+    return [calls[k] for k in DEALT]
 
 
 def rank_program(g, core, T, topo):
     rank = T.rank_of(core)
     if rank is None:
         return
-    Q = {"v": g.vector, "a": g.scalar, "p": g.tensor, "g": g, "s": g.sync}
-    CS = {"v": "cv", "a": "ca", "p": "cp", "g": "cg"}
-    count = {"v": 0, "a": 0, "p": 0, "g": 0}
-    known = {e: {} for e in Q}
-    wrote, read, bank = {}, {}, {}
-    totals = {}
-
-    def wait_for(e, events):
-        for sem, n, clock in sorted(events, key=lambda ev: -ev[1]):
-            if known[e].get(sem, 0) < n:
-                Q[e].wait_ge(T.sem[sem], n)
-                known[e][sem] = n
-                for k, m in clock.items():
-                    known[e][k] = max(known[e].get(k, 0), m)
-
-    def before(e, rd, wr, ps):
-        ev = [wrote[r] for r in rd if r in wrote]
-        for w in wr:
-            ev += read.get(w, []) + ([wrote[w]] if w in wrote else [])
-        for b in ps:
-            ev += [x for q, x in bank.get(b, {}).items() if q != e]
-        if e == "p":
-            ev = [x for x in ev if x[0] != "cp"]
-        wait_for(e, ev)
-
-    def after(e, ev, rd, wr, ps):
-        for r in rd:
-            read.setdefault(r, []).append(ev)
-        for w in wr:
-            wrote[w] = ev
-            read[w] = []
-        for b in ps:
-            bank.setdefault(b, {})[e] = ev
-        totals[ev[0]] = max(totals.get(ev[0], 0), ev[1])
-
-    def op(e, make, rd, wr, ps=()):
-        before(e, rd, wr, ps)
-        count[e] += 1
-        make().then_inc(T.sem[CS[e]], 1)
-        after(e, (CS[e], count[e], dict(known[e])), rd, wr, ps)
-
-    def dma(e, sem, out, in_, rd, wr):
-        before(e, rd, wr, ())
-        Q[e].dma_start(out, in_).then_inc(T.sem[sem], 16)
-        after(e, (sem, 16, dict(known[e])), rd, wr, ())
-
     v, act, pe = g.vector, g.scalar, g.tensor
+    calls = []
 
-    def ts(out, in0, s1, op0, s2, op1, rd, wr, ps=()):
+    def call(e, busy, make, rd, wr, ps=(), way=0, sem=None, n=1):
+        calls.append(dict(e=e, busy=busy, make=make, rd=list(rd), wr=list(wr), ps=ps, way=way, sem=sem, n=n))
+
+    def vop(make, rd, wr, ps=(), c=128):
+        call("v", START + max(64, c), make, rd, wr, ps)
+
+    def ts(out, in0, s1, op0, s2, op1, rd, wr, ps=(), c=128):
         if op1 is None:
-            op("v", lambda: v.tensor_scalar(out, in0, s1, None, op0), rd, wr, ps)
+            vop(lambda: v.tensor_scalar(out, in0, s1, None, op0), rd, wr, ps, c)
         else:
-            op("v", lambda: v.tensor_scalar(out, in0, s1, s2, op0, op1), rd, wr, ps)
+            vop(lambda: v.tensor_scalar(out, in0, s1, s2, op0, op1), rd, wr, ps, c)
 
-    def tt(out, in0, in1, o, rd, wr, ps=()):
-        op("v", lambda: v.tensor_tensor(out, in0, in1, o), rd, wr, ps)
+    def tt(out, in0, in1, o, rd, wr, ps=(), c=128):
+        vop(lambda: v.tensor_tensor(out, in0, in1, o), rd, wr, ps, c)
 
-    def cp(out, in_, rd, wr, ps=()):
-        op("v", lambda: v.tensor_copy(out, in_), rd, wr, ps)
+    def cp(out, in_, rd, wr, ps=(), c=128):
+        vop(lambda: v.tensor_copy(out, in_), rd, wr, ps, c)
 
-    def ms(ap, c, wr):
-        op("v", lambda: v.memset(ap, c), (), wr)
+    def ac(out, in_, func, bias, scale, rd, wr, ps=(), c=128):
+        call("a", ASTART + c, lambda: act.activation(out, in_, func, bias=bias, scale=scale), rd, wr, ps)
 
-    def ac(out, in_, func, bias, scale, rd, wr, ps=()):
-        op("a", lambda: act.activation(out, in_, func, bias=bias, scale=scale), rd, wr, ps)
-
-    def mm(out, lhsT, rhs, start, stop, rd, wr, ps):
-        op("p", lambda: pe.matmul(out, lhsT, rhs, start, stop), rd, wr, ps)
-
-    def gather(e, out, win, off, rd, wr):
-        if e == "v":
-            cp(out, win.indirect(off), rd, wr)
+    def lin(on, out, in_, scale, bias, rd, wr, ps=(), n=128, narrow=False):
+        if on == "a":
+            ac(out, in_, AF.Identity, bias, scale, rd, wr, ps, n)
         else:
-            ac(out, win.indirect(off), AF.Identity, 0.0, 1.0, rd, wr)
+            ts(out, in_, scale, A.mult, bias, A.add, rd, wr, ps, n // 2 if narrow else n)
 
-    sent = [0]
+    def gather(on, out, win, off, n, rd, wr):
+        if on == "a":
+            ac(out, win.indirect(off), AF.Identity, 0.0, 1.0, rd, wr, (), GATHER * n - 120)
+        else:
+            cp(out, win.indirect(off), rd, wr, (), GATHER * n)
 
-    def send(sem, h, step, src, dst, rd, wr):
-        before("g", rd, (), ())
-        tr = []
-        for j, s in enumerate(HALF[h]):
-            to = T.cores[(rank + step * (s + 4)) % N]
-            rid, pid, _ = topo.addr(to)
-            mask = sum(1 << e for e in topo.engines(core, to)[j::4])
-            tr.append(RemoteDMATransfer(dst_ids=[DstId(rid=rid, pnc=pid)], dma_engine_mask=mask,
-                                        remote_sem=T.sem[sem], src=src(s), dst=dst(s)))
-        g.remote_dma_fused(tr, local_sem=T.sem.snd)
-        sent[0] += 4 * len(tr)
-        wrote[wr] = (sem, 4 * len(tr), {})
-        totals[sem] = 4 * len(tr)
+    def mm(out, lhsT, rhs, start, stop, rd, reg, b, c=128):
+        ends = start or stop
+        call("p", c // 2, lambda: pe.matmul(out, lhsT, rhs, start, stop), rd + ([] if ends else [reg, "open " + b]),
+             [reg, "open " + b] if ends else [], (b,))
 
-    dma("s", "lnx", T.npi[:, 0:128], T.nxt[:], (), ["nxi"])
-    dma("s", "lpri", T.prii[:], T.pri[:], (), ["prii"])
-    dma("s", "lx", T.xs[:], T.x[:], (), ["xs"])
-    dma("s", "lkey", T.keyi[:], T.key[:], (), ["keyi"])
-    dma("s", "lw", T.ws[:, 0:5], T.w[:], (), ["ws"])
-    dma("s", "lrw", T.rwi[:], T.rw[:], (), ["rwi"])
-    dma("s", "lpv", T.npi[:, 128:256], T.prv[:], (), ["pvi"])
-    dma("s", "lv0", T.vs[:, 0:V // 2], T.val[:, 0:V // 2], (), ["vs0"])
+    def dma(e, sem, out, in_, rd, wr, way):
+        call(e, 60, lambda: {"s": g.sync, "a": act}[e].dma_start(out, in_), rd, wr, (), LOAD + way, sem, 16)
+
+    def send(sem, h, step, src, dst, rd, wr, way, first=False):
+        def make():
+            tr = []
+            for j, s in enumerate(HALF[h]):
+                to = T.cores[(rank + step * (s + 4)) % N]
+                rid, pid, _ = topo.addr(to)
+                mask = sum(1 << x for x in topo.engines(core, to)[j::4])
+                tr.append(RemoteDMATransfer(dst_ids=[DstId(rid=rid, pnc=pid)], dma_engine_mask=mask,
+                                            remote_sem=T.sem[sem], src=src(s), dst=dst(s)))
+            g.remote_dma_fused(tr, local_sem=T.sem.snd)
+        call("g", ISSUE + FIRST * first, make, rd, wr, (), FLIGHT - ISSUE + way, sem, -4 * len(HALF[h]))
 
     def iota(out, pattern, base, cm, wr, fl=True):
+        n = math.prod(c for _, c in pattern)
         if fl:
-            op("g", lambda: g.iota(out, pattern, base, cm, allow_small_or_imprecise_dtypes=True), (), wr)
+            call("g", 160 + 2 * n, lambda: g.iota(out, pattern, base, cm, allow_small_or_imprecise_dtypes=True), (), wr)
         else:
-            op("g", lambda: g.iota(out, pattern, base, cm), (), wr)
-    iota(T.kci[:, 0:1], [[1, 1]], 0, 1, ["kc0"], False)
-    iota(T.j8[:], [[1, 8]], 0, 0, ["j8"])
-    iota(T.dif[:], [[1, 128]], 0, -1, ["dif"])
-    iota(T.c240[:], [[1, 240]], -112, 0, ["c240"])
-    iota(T.m16[:], [[1, 8], [0, 16]], 0, 0, ["m16"])
-    iota(T.a16[:], [[0, 8], [16, 8]], 0, 0, ["a16"], False)
-    iota(T.b0[:], [[0, F]], 0, 0, ["b0h", "b0l"])
+            call("g", 160 + 2 * n, lambda: g.iota(out, pattern, base, cm), (), wr)
 
-    ms(T.rst[:], 1.0, ["rst"])
-    ms(T.gw[:], 0.0, ["gmf", "gmn"])
-    ms(T.zb[:], 0.0, ["zb"])
-    ms(T.pp[:, 0:16], 0.0, ["pp0"])
-    ts(T.kti[:, 0:1], T.kci[:, 0:1], 15, A.bitwise_and, None, None, ["kc0"], ["kt0"])
-    ts(T.kti[:, 1:2], T.kci[:, 0:1], 4, A.arith_shift_right, None, None, ["kc0"], ["kt1"])
-    ts(T.kti[:, 2:3], T.kci[:, 0:1], 7, A.bitwise_and, None, None, ["kc0"], ["kt2"])
-    ts(T.kti[:, 3:4], T.kci[:, 0:1], 3, A.arith_shift_right, 3, A.bitwise_and, ["kc0"], ["kt3"])
-    ms(T.rst[:, 0:128:16], 0.0, ["rst"])
-    cp(T.ktf[:], T.kti[:], ["kt0", "kt1", "kt2", "kt3"], ["ktf"])
-    kmod, kdiv, k7, k3 = T.ktf[:, 0:1], T.ktf[:, 1:2], T.ktf[:, 2:3], T.ktf[:, 3:4]
-    gmf = T.gw[:, 24:32]
-    ts(T.um[:], T.dif[:], 0.0, A.is_ge, None, None, ["dif"], ["um"])
-    ts(gmf, T.j8[:], kdiv, A.is_equal, None, None, ["j8", "ktf"], ["gmf"])
-    ts(T.gw[:, 16:24], T.j8[:], kdiv, A.is_equal, -1.0, A.mult, ["j8", "ktf"], ["gmn"])
-    ts(T.col[:, 0:1], kmod, -4.0 * W, A.add, None, None, ["ktf"], ["col0"])
-    ts(T.col[:, 1:2], kmod, 128.0, A.mult, None, None, ["ktf"], ["col1"])
-    ts(T.lm[:], T.dif[:], 0.0, A.is_lt, None, None, ["dif"], ["lm"])
-    ts(T.idf[:], T.dif[:], 0.0, A.is_equal, None, None, ["dif"], ["idf"])
-    ts(T.em[:], T.c240[:], kmod, A.is_equal, None, None, ["c240", "ktf"], ["em"])
-    ts(T.nl[:], T.dif[:], 0.0, A.is_lt, -1.0, A.mult, ["dif"], ["nl"])
-    ts(T.idk[:], T.dif[:], 0.0, A.is_equal, 1024.0, A.mult, ["dif"], ["idk"])
-    ac(T.wex[:, 0:1], k3, AF.Exp, 3.0 * LN64, -LN64, ["ktf"], ["wex0"])
-    ac(T.wex[:, 1:2], k3, AF.Exp, 0.0, LN64, ["ktf"], ["wex1"])
-    ac(T.col[:, 2:4], T.wex[:], AF.Identity, 0.0, 1.0, ["wex0", "wex1"], ["col2"])
-    ac(T.idb[:], T.idf[:], AF.Identity, 0.0, 1.0, ["idf"], ["idb"])
-    ac(T.gmb[:], gmf, AF.Identity, 0.0, 1.0, ["gmf"], ["gmb"])
+    def select(out, in_, pattern, test, fill, base, cm, rd, wr):
+        n = math.prod(c for _, c in pattern)
+        call("g", 200 + 2 * n, lambda: g.affine_select(out, in_, pattern, test, float(fill), base, cm), rd, wr)
+
+    def band(name, c, test=A.not_equal):
+        select(T[name][:], T.zb[:], [[1, 128]], test, c, 0, -1, ["zb"], [name])
+
+    def group_mask(out, zeros, pattern, c, rd, wr):
+        select(out, zeros, pattern, A.is_gt, c, 0, -1, rd, wr)
+        select(out, out, pattern, A.is_ge, 0, 15, -1, [], wr)
+
+    def col(j):
+        return T.col[:, j:j + 1]
 
     P = T.pp[:, 16:144]
-    cp(T.npu[:, 0:128], T.npi[:, 0:128], ["nxi"], ["nxu"])
-    cp(T.prb[:], T.prii[:], ["prii"], ["prb"])
-    cp(T.gmh[:], gmf, ["gmf"], ["gmh"])
-    for j in range(8):
-        ts(T.gx[:, 128 * j:128 * j + 128], T.prb[:], T.gw[:, 24 + j:25 + j], A.mult, None, None, ["prb", "gmf"], ["gx%d" % j])
-    for j in range(8):
-        mm(T.qs[:, 0:128], T.em[:, 112 - 16 * j:240 - 16 * j], T.gx[:, j:1024:8], j == 0, j == 7,
-           ["em"] + ["gx%d" % k for k in range(8)], ["qs0"], ["qs"])
-    gather("a", T.x1[:], T.xs[:, 0:F], T.npu[:, 0:128], ["xs", "nxu"], ["x1"])
-    for k in range(2):
-        ts(T.pk[:, 128 * k:128 * k + 128], T.m16[:], k7, A.is_equal, T.col[:, 2 + k:3 + k], A.mult, ["m16", "ktf", "col2"], ["pk%d" % k])
-    cp(T.keyf[:], T.keyi[:], ["keyi"], ["keyf"])
-    op("p", lambda: pe.transpose(T.qk[:, 0:128], T.keyf[:], T.idf[:]), ["keyf", "idf"], ["qk1"], ["qk"])
-    cp(P, T.qs[:, 0:128], ["qs0"], ["pp"], ["qs"])
-    for d in range(5):
-        ts(T.dg[:, 128 * (5 * OWN + d):128 * (5 * OWN + d) + 128], T.idb[:], T.ws[:, d:d + 1], A.mult, None, None,
-           ["idb", "ws"], ["dgo%d" % d])
-    ts(T.qv[:, 0:128], T.qk[:, 0:128], 16.0, A.mult, T.col[:, 0:1], A.add, ["qk1", "col0"], ["base"], ["qk", "qv"])
-    ts(T.rti[:, 0:128], T.rwi[:], 5, A.arith_shift_right, None, None, ["rwi"], ["rt0"])
-    ts(T.rti[:, 128:256], T.rwi[:], 31, A.bitwise_and, None, None, ["rwi"], ["rt1"])
-    cp(T.npu[:, 128:256], T.npi[:, 128:256], ["pvi"], ["pvu"])
-    ts(T.rtb[:, 0:128], T.rti[:, 0:128], 32.0, A.mult, None, None, ["rt0"], ["rb0"])
-    cp(T.rtb[:, 128:256], T.rti[:, 128:256], ["rt1"], ["rb1"])
-    gather("a", T.xm1[:], T.xs[:, 0:F], T.npu[:, 128:256], ["xs", "pvu"], ["xm1"])
-    dma("s", "lb0", T.b0[0:128:16, :], T.rtb[:, 0:128], ["rb0"], ["b0h"])
-    dma("s", "lb1", T.b0[1:128:16, :], T.rtb[:, 128:256], ["rb1"], ["b0l"])
-    dma("s", "lv1", T.vs[:, V // 2:V], T.val[:, V // 2:V], (), ["vs1"])
+    gmf = T.gw[:, 24:32]
+    kmod, ka, ks4, k3, k128, kdiv = (T.ktf[:, k:k + 1] for k in range(6))
+    z1, tv = T.qv[:, 128:256], T.qv[:, 256:384]
+    pq, cst = T.qa[:, 256:384], T.qa[:, 384:512]
+    C0 = (512, 0)
+    TAB = ["xm2", "xm1", "xs", "x1", "x2", "r3"]
 
-    samp, tv, cst = T.qv[:, 128:256], T.qv[:, 256:384], T.qv[:, 384:512]
-    QK = [(T.qd, 256, "qd"), (T.qk, 0, "qk")]
-    QH = [(T.qh0, "qh0"), (T.qh1, "qh1")]
-    QE = [(T.qe, "qe"), (T.qs, "qs")]
+    def fields():
+        iota(T.kci[:, 0:1], [[1, 1]], 0, 1, ["kc0"], False)
+        iota(T.dif[:], [[1, 128]], 0, -1, ["dif"])
+        iota(T.kci[:, 1:2], [[1, 1]], 0, 128, ["kc1"], False)
+        iota(T.j8[:], [[1, 8]], 0, 0, ["j8"])
+        iota(T.c240[:], [[1, 240]], -112, 0, ["c240"])
+        for ap, x, reg in ((T.zb[:], 0.0, "zb"), (T.gw[:], 0.0, "gw"), (T.rst[:], 1.0, "rst")):
+            vop(lambda ap=ap, x=x: v.memset(ap, x), (), [reg], c=64)
+        vop(lambda: v.memset(T.b0[:, 0:1024], 0.0), (), ["b0z"], c=512)
+        for j, c, shift, mask in ((2, 0, 5, 3), (5, 0, 4, 7), (0, 0, 0, 15), (1, 0, 2, 7), (3, 0, 0, 3), (4, 1, 0, 15 * 128)):
+            ts(T.kti[:, j:j + 1], T.kci[:, c:c + 1], shift, A.arith_shift_right, mask, A.bitwise_and, ["kc%d" % c], ["kt%d" % j], c=1)
+        cp(T.ktf[:], T.kti[:], ["kt%d" % k for k in range(6)], ["ktf"], c=6)
+        ts(T.idb[:], T.dif[:], 0.0, A.is_equal, None, None, ["dif"], ["idb"], c=64)
+        ts(gmf, T.j8[:], kdiv, A.is_equal, None, None, ["j8", "ktf", "gw"], ["gmf"], c=8)
+        vop(lambda: v.memset(T.b0[:, 1024:F], 0.0), ["b0z"], ["b0h", "b0l"], c=512)
+        ts(T.em[:], T.c240[:], kmod, A.is_equal, None, None, ["c240", "ktf"], ["em"])
+        vop(lambda: v.memset(T.rst[:, 0:128:16], 0.0), (), ["rst"], c=8)
 
-    def forward(a, relus):
-        mm(T.qd[:, 128:256], T.idk[:], P, True, True, ["idk", "pp"], ["p1k"], ["qd"])
-        mm(T.qd[:, 0:128], T.um[:], P, True, False, ["um", "pp"], ["dd"], ["qd"])
-        mm(T.qd[:, 0:128], T.lm[:], T.pp[:, 15:143], False, False, ["lm", "pp", "pp0"], ["dd"], ["qd"])
-        mm(T.qd[:, 16:128:16], T.nl[:], T.pp[:, 31:143:16], False, True, ["nl", "pp"], ["dd"], ["qd"])
-        op("v", lambda: v.tensor_tensor_scan(T.sm[:], T.rst[:], T.qd[:, 0:128], 0.0, A.mult, A.add), ["rst", "dd"], ["sm"], ["qd"])
-        ts(T.si[:], T.sm[:], 1024.0, A.mult, (-rank - 5) % N * W, A.add, ["sm"], ["si"])
-        ts(T.low[:], T.si[:], 127 << 10, A.bitwise_and, None, None, ["si"], ["low"])
-        ts(T.t1[:], T.si[:], 7 << 17, A.bitwise_and, None, None, ["si"], ["t1"])
-        tt(samp, T.low[:], T.qd[:, 128:256], A.is_lt, ["low", "p1k"], ["samp"], ["qd", "qv"])
-        tt(T.z1[:], T.t1[:], T.qv[:, 0:128], A.add, ["t1", "base"], ["z1"], ["qv"])
-        tt(T.zz[:], T.z1[:], samp, A.mult, ["z1", "samp"], ["zz"], ["qv"])
-        for s in range(N):
-            lo, out = (s - 4) * W, T.cl[:, 128 * s:128 * s + 128]
-            if s < 4:
-                ts(out, T.zz[:], lo, A.max, lo + W, A.min, ["zz"], ["cl%d" % s])
-                mm(T.qd[:, 256 + 8 * s:264 + 8 * s], out, gmf, True, True, ["cl%d" % s, "gmf"], ["qk0"], ["qd"])
-                continue
-            if relus == "a":
-                ac(out, T.zz[:], AF.Relu, -lo, 1.0, ["zz"], ["cl%d" % s])
+    def masks():
+        select(T.um[:], T.zb[:], [[-1, 128]], A.is_gt, 8192, 0, 1, ["zb"], ["um"])
+        band("lm", 8192.0, A.is_ge), band("nl", -8192.0, A.is_ge), band("i32", 32.0)
+        iota(T.turn[:], [[0, 8]], (-rank - 5) % N * W // 32, 0, ["turn"])
+        iota(col(0), [[1, 1]], -4 * W, 1, ["col0"])
+        iota(T.pp[:, 0:16], [[0, 16]], 0, 0, ["pad"])
+        group_mask(T.gw[:, 16:24], T.gw[:, 16:24], [[16, 8]], -1, ["gw"], ["gmn"])
+        iota(T.m16[:], [[1, 8], [0, 16]], 0, 0, ["m16"])
+        band("nid", -1.0)
+        select(T.ma[0:4, :], T.zb[0:4, :], [[0, 32], [1, 4]], A.not_equal, 1, 0, -1, ["zb"], ["ma"])
+        select(T.mb[0:4, :], T.zb[0:4, :], [[0, 8], [1, 4], [0, 4]], A.is_equal, 32768, 0, -1, ["zb"], ["mb"])
+        group_mask(T.g1[:], T.zb[:, 0:32], [[16, 8], [0, 4]], 1, ["zb"], ["g1"])
+
+    def diagonals():
+        for d in range(ND):
+            c0 = 128 * (ND * OWN + d)
+            lin("v", T.dg[:, c0:c0 + 128], T.idb[:], T.ws[:, d:d + 1], 0.0, ["idb", "wi"], ["dg%d_%d" % (OWN, d)], narrow=True)
+
+    def matrices(h):
+        send("wa%d" % h, h, -1, lambda s: T.dg[:, 128 * ND * OWN:128 * ND * (OWN + 1)], lambda s: T.dg[:, 128 * ND * s:128 * ND * (s + 1)],
+             ["dg%d_%d" % (OWN, d) for d in range(ND)], ["dg%d_%d" % (s, d) for s in HALF[h] for d in range(ND)], 1000)
+
+    def rewards():
+        ts(T.rti[:, 0:128], T.rwi[:], -32, A.bitwise_and, None, None, ["rwi"], ["rt0"])
+        ts(T.rti[:, 128:256], T.rwi[:], 31, A.bitwise_and, None, None, ["rwi"], ["rt1"])
+        cp(T.rtb[:], T.rti[:], ["rt0", "rt1"], ["rtb"], c=256)
+        dma("s", "lb0", T.b0[0:128:16, :], T.rtb[:, 0:128], ["rtb"], ["b0h"], 1200)
+        dma("s", "lb1", T.b0[1:128:16, :], T.rtb[:, 128:256], ["rtb"], ["b0l"], 1500)
+        dma("s", "lv1", T.vs[:, V // 2:V], T.val[:, V // 2:V], (), ["vs1"], 6000)
+
+    def regroup(out, src, rd, reg, b):
+        for j in range(8):
+            mm(out, T.em[:, 112 - 16 * j:240 - 16 * j], src(j), j == 0, j == 7, ["em"] + rd, reg, b)
+
+    def pointers():
+        ts(T.npb[:], T.npi[:], 7, A.arith_shift_right, None, None, ["nxi", "pvi"], ["npb"], c=256)
+        ts(T.qh0[:, 0:256], T.npb[:], -2047.0 / 16.0, A.mult, None, None, ["npb"], ["qh0"], ["qh0"], 256)
+        tt(T.npf[:], T.npi[:], T.qh0[:, 0:256], A.add, ["nxi", "pvi", "qh0"], ["npf"], ["qh0"], 256)
+        ts(T.ppu[:], T.npf[:], 16.0, A.mult, None, None, ["npf"], ["ppu0", "ppu128"], c=256)
+
+    def state():
+        cp(T.prb[:], T.prii[:], ["prii"], ["prb"])
+        for j in range(8):
+            lin("v", T.gx[:, 128 * j:128 * j + 128], T.prb[:], T.gw[:, 24 + j:25 + j], 0.0, ["prb", "gmf"], ["gx%d" % j], narrow=True)
+        regroup(T.qd[:, 128:256], lambda j: T.gx[:, j:1024:8], ["gx%d" % j for j in range(8)], "p0", "qd")
+
+    def keys():
+        cp(T.keyf[:], T.keyi[:], ["keyi"], ["keyf"])
+        mm(T.qk[:, 0:128], T.keyf[:], T.idf[:], True, True, ["keyf", "idf"], "kt", "qk", 512)
+        lin("v", P, T.qd[:, 128:256], 1.0, 0.0, ["p0"], ["pp"], ["qd"])
+        lin("v", T.qv[:, 0:128], T.qk[:, 0:128], 128.0, col(0), ["kt", "col0"], ["base"], ["qk", "qv"])
+
+    def step(name, src, off, c0):
+        gather("a", T[name][:], T[src][:, 0:F], T[off][:, c0:c0 + 128], F, [src, off + str(c0)], [name])
+
+    def reward_step(name, src, off, rd):
+        tt(T[name][:], T[src][:, 0:F].indirect(T[off][:, 0:128]), T.b1[:], A.add, rd + ["b1_%d" % i for i in range(16)] + [off + "0"],
+           [name], c=GATHER * F)
+
+    def running():
+        mm(T.qd[:, 0:128], T.um[:], P, True, False, ["um", "pp"], "dd", "qd")
+        mm(T.qd[:, 0:128:16], T.i32[:], T.turn[:], False, False, ["i32", "turn"], "dd", "qd", 64)
+        mm(T.qd[:, 0:128], T.lm[:], T.pp[:, 15:143], False, False, ["lm", "pp", "pad"], "dd", "qd")
+        mm(T.qd[:, 16:128:16], T.nl[:], T.pp[:, 31:143:16], False, True, ["nl", "pp"], "dd", "qd", 64)
+        mm(pq, T.idb[:], P, True, True, ["idb", "pp"], "pq", "qa")
+
+    def forward(a, on_scalar):
+        vop(lambda: v.tensor_tensor_scan(T.si[:], T.rst[:], T.qd[:, 0:128], 0.0, A.mult, A.add), ["rst", "dd"], ["si"], ["qd"])
+        ts(T.low[:], T.si[:], 13, A.arith_shift_right, 127, A.bitwise_and, ["si"], ["low"])
+        ts(T.t1[:], T.si[:], 7 << 20, A.bitwise_and, None, None, ["si"], ["t1"])
+        tt(T.samp[:], T.low[:], pq, A.is_lt, ["low", "pq"], ["samp"], ["qa"])
+        tt(z1, T.t1[:], T.qv[:, 0:128], A.add, ["t1", "base"], ["z1"], ["qv"])
+        tt(T.zz[:], z1, T.samp[:], A.mult, ["z1", "samp"], ["zz"], ["qv"])
+        cl = lambda h, j: T.cl[:, 512 * h + 128 * j:512 * h + 128 * j + 128]
+        todo = [(0, 0), (1, 0), (0, 1), (0, 2), (1, 1), (0, 3), (1, 2), (1, 3)]
+        for h, j in todo:
+            if h == 0:
+                ts(cl(h, j), T.zz[:], float(j * W), A.add, 0.0, A.min, ["zz"], ["cl%d_%d" % (h, j)])
+            elif j < on_scalar:
+                ac(cl(h, j), T.zz[:], AF.Relu, -float(j * W), 1.0, ["zz"], ["cl%d_%d" % (h, j)])
             else:
-                ts(out, T.zz[:], -lo, A.add, 0.0, A.max, ["zz"], ["cl%d" % s])
-            mm(T.qk[:, 0:32], out, T.gw[:, 56 - 8 * s:88 - 8 * s], s == 4, s == 7, ["cl%d" % s, "gmf", "gmn"], ["qk1"], ["qk"])
-
-        def ask(h, between):
-            buf, c0, b = QK[h]
-            c = slice(32 * h, 32 * h + 32)
-            cp(T.ki[:, c], buf[:, c0:c0 + 32], ["qk%d" % h], ["ki%d" % h], [b])
-            ts(T.ks[:, c], T.ki[:, c], 4, A.arith_shift_right, V - 1, A.bitwise_and, ["ki%d" % h], ["ks%d" % h])
-            between()
-            k0 = RQ * a + 8 * kept(4 * h)
-            cp(T.rq[:, k0:k0 + 32], T.ks[:, c], ["ks%d" % h], ["ku%d_%d" % (a, h)])
-            send("rq%d_%d" % (a, h), h, 1, lambda s: T.rq[:, RQ * a + 8 * kept(s):RQ * a + 8 * kept(s) + 8],
-                 lambda s: T.rq[:, RQ * a + 8 * asked(s):RQ * a + 8 * asked(s) + 8], ["ku%d_%d" % (a, h)], "req%d_%d" % (a, h))
-        ts(T.uu[:], T.t1[:], 1.0 / W, A.mult, -3.5, A.add, ["t1"], ["uu"])
-        ask(0, lambda: tt(T.zc[:], T.uu[:], samp, A.mult, ["uu", "samp"], ["zc"], ["qv"]))
-        ask(1, lambda: ts(T.pl[:], T.ki[:], 15, A.bitwise_and, None, None, ["ki0", "ki1"], ["pl"]))
-        tt(T.kk[:], T.pl[:], T.a16[:], A.add, ["pl", "a16"], ["kk"])
-        ts(T.tp[:], T.kk[:], 16.0, A.mult, kmod, A.add, ["kk", "ktf"], ["tp"])
-        ts(T.tu[:], T.kk[:], T.col[:, 1:2], A.add, None, None, ["kk", "col1"], ["tu"])
-
-    def scales_1():
-        ac(T.c1[:], P, AF.Identity, 32.0, -1.0, ["pp"], ["c1"])
-        ac(T.ua[:], T.zc[:], AF.Abs, 0.0, 1.0, ["zc"], ["ua"])
-        ac(T.sg[:], T.zc[:], AF.Sign, 0.0, 1.0, ["zc"], ["sg"])
-        ac(T.e1[:], T.ua[:], AF.Exp, 0.5 * LN64, -LN64, ["ua"], ["e1"])
-
-    def scales_2():
-        tt(T.c2[:], T.c1[:], samp, A.mult, ["c1", "samp"], ["c2"], ["qv"])
-        tt(T.es[:], T.e1[:], T.sg[:], A.mult, ["e1", "sg"], ["es"])
-        tt(cst, T.c2[:], P, A.add, ["c2", "pp"], ["cst"], ["qv"])
-
-    def scales_3():
-        ac(T.sa[:], T.es[:], AF.Relu, 0.0, -1.0, ["es"], ["sa"])
-        ac(T.sb[:], T.es[:], AF.Relu, 0.0, 1.0, ["es"], ["sb"])
-
-    TAB = {0: (T.xm2, "xm2"), 1: (T.xm1, "xm1"), 2: (T.xs, "xs"), 3: (T.x1, "x1"), 4: (T.x2, "x2"), 5: (T.rwt, "rwt")}
-
-    def pick(e, d, h, last=False):
-        tab, name = TAB[d]
-        off, on = (T.tu, "tu") if d == 2 else (T.tp, "tp")
-        c0 = 1024 * d + 512 * h
-        gather(e, T.xg[:, c0:c0 + 512], tab[:, 0:F], off[:, 32 * h:32 * h + 32], [name, on], ["g%d_%d" % (d, h)])
-        if d == 5:
-            for i in range(16):
-                mm(QE[h][0][0:32, i:128:16], T.xg[:, c0 + i:c0 + 512:16], T.gmb[:], False, False,
-                   ["g5_%d" % h, "gmb"], ["qe%d" % h], [QE[h][1]])
-            return
-        for k in range(4):
-            s = 4 * h + k
-            mm(QH[h][0][:, 128 * k:128 * k + 128], T.dg[:, 128 * (5 * s + d):128 * (5 * s + d) + 128],
-               T.xg[:, c0 + 128 * k:c0 + 128 * k + 128], False, last and k == 3,
-               ["dg%d" % h, "dgo%d" % d, "g%d_%d" % (d, h)], ["qh%d" % h], [QH[h][1]])
-
-    def serve(a, e, h):
-        c0 = VR * a + 512 * h
-        gather(e, T.vr[:, c0:c0 + 512], T.vs[:, 0:V], T.rq[:, RQ * a + 32 * h:RQ * a + 32 * h + 32],
-               ["vs0", "vs1", "req%d_%d" % (a, h)] + ["ku%d_1" % a] * h, ["vg%d_%d" % (a, h)])
-        send("rt%d_%d" % (a, h), h, -1, lambda s: T.vr[:, VR * a + 128 * asked(s):VR * a + 128 * asked(s) + 128],
-             lambda s: T.vr[:, VR * a + 128 * kept(s):VR * a + 128 * kept(s) + 128], ["vg%d_%d" % (a, h)], "ret%d_%d" % (a, h))
-
-    def open_sums():
+                ts(cl(h, j), T.zz[:], -float(j * W), A.add, 0.0, A.max, ["zz"], ["cl%d_%d" % (h, j)])
+        for h, j in todo:
+            c0 = 256 + C0[h] // 16
+            mm(T.qd[:, c0:c0 + 32], cl(h, j), T.gw[:, 24 - 8 * j:56 - 8 * j], (h, j) == todo[0], (h, j) == todo[-1],
+               ["cl%d_%d" % (h, j), "gmf", "gmn"], "pick", "qd", 256)
+        ts(T.uu[:], T.t1[:], 1.0 / (8 * W), A.mult, -3.5 / 8, A.add, ["t1"], ["uu"])
+        kept_priorities()
+        cp(T.ki[:], T.qd[:, 256:320], ["pick"], ["ki"], ["qd"], 64)
+        ts(T.ks[:], T.ki[:], 7, A.arith_shift_right, V - 1, A.bitwise_and, ["ki"], ["ks"], c=64)
+        ts(T.pl[:], T.ki[:], 127, A.bitwise_and, None, None, ["ki"], ["pl"], c=64)
+        cp(T.rq[:, RQ * a + 56:RQ * a + 120], T.ks[:], ["ks"], ["ku%d" % a], c=64)
         for h in range(2):
-            mm(QH[h][0][:], T.zb[:], T.xs[:, 0:512], True, False, ["zb", "xs"], ["qh%d" % h], [QH[h][1]])
-            mm(QE[h][0][0:32, 0:128], T.zb[:, 0:32], T.zb[:], True, False, ["zb"], ["qe%d" % h, "qs0"], [QE[h][1]])
+            send("rq%d_%d" % (a, h), h, 1, lambda s: T.rq[:, RQ * a + 8 * kept(s):RQ * a + 8 * kept(s) + 8],
+                 lambda s: T.rq[:, RQ * a + 8 * asked(s):RQ * a + 8 * asked(s) + 8], ["ku%d" % a], ["req%d_%d" % (a, h)], 0, a == h == 0)
+        ts(T.tp[:], T.pl[:], 16.0, A.mult, kmod, A.add, ["pl", "ktf"], ["tp"], c=64)
+        ts(T.tu[:], T.pl[:], k128, A.add, None, None, ["pl", "ktf"], ["tu"], c=64)
 
-    def errors(a, h):
-        r0 = VR * a + 128 * kept(4 * h)
-        for c in range(2):
-            c0 = 512 * h + 256 * c
-            tt(T.prod[:, c0:c0 + 256], QH[h][0][:, c:512:2], T.vr[:, r0 + c:r0 + 512:2], A.mult,
-               ["qh%d" % h, "ret%d_%d" % (a, h)] + ["vg%d_1" % a] * h, ["pr%d_%d" % (h, c)], [QH[h][1]])
-            for i in range(c, 16, 2):
-                mm(QE[h][0][0:32, i:128:16], T.prod[:, c0 + i // 2:c0 + 256:8], T.gmh[:], False, i == 15,
-                   ["pr%d_%d" % (h, c), "gmh"], ["qe%d" % h], [QE[h][1]])
+    def scales():
+        for k, m in enumerate(("idb", "nid")):
+            out = T.qk[:, 128 + 128 * k:256 + 128 * k]
+            mm(out, T[m][:], T.uu[:], True, False, [m, "uu"], "y%d" % k, "qk")
+            mm(out, T.nid[:], T.samp[:], False, True, ["nid", "samp"], "y%d" % k, "qk")
+        ac(T.sab[:], T.qk[:, 128:384], AF.Exp, -11.5 * LN64, -8.0 * LN64, ["y0", "y1"], ["sab"], ["qk"], 256)
 
-    def sizes(h):
-        ac(T.ea[0:32, 128 * h:128 * h + 128], QE[h][0][0:32, 0:128], AF.Abs, 0.0, 0.0625, ["qe%d" % h], ["ea%d" % h], [QE[h][1]])
+    def kept_priorities():
+        tt(T.dp[:], T.samp[:], pq, A.mult, ["samp", "pq"], ["dp"], ["qa"])
+        mm(cst, T.idb[:], P, True, False, ["idb", "pp"], "cst", "qa")
+        mm(cst, T.i32[:], T.samp[:], False, False, ["i32", "samp"], "cst", "qa")
+        mm(cst, T.nid[:], T.dp[:], False, True, ["nid", "dp"], "cst", "qa")
+
+    def serve(a, h, on):
+        c0 = VR * a + 512 * h
+        gather(on, T.vr[:, c0:c0 + 512], T.vs[:, 0:V], T.rq[:, RQ * a + 32 * h:RQ * a + 32 * h + 32], 512,
+               ["vs0", "vs1", "req%d_%d" % (a, h)] + ["ku%d" % a] * h, ["vg%d_%d" % (a, h)])
+        send("rt%d_%d" % (a, h), h, -1, lambda s: T.vr[:, VR * a + 128 * asked(s):VR * a + 128 * asked(s) + 128],
+             lambda s: T.vr[:, VR * a + 128 * kept(s):VR * a + 128 * kept(s) + 128], ["vg%d_%d" % (a, h)], ["ret%d_%d" % (a, h)], 400)
+
+    def part(d, on, halves=(0, 1)):
+        c0, n, off = min(C0[h] for h in halves), 512 * len(halves), "tu" if d == 2 else "tp"
+        gather(on, T.xg[:, 1024 * d + c0:1024 * d + c0 + n], T[TAB[d]][:, 0:F], T[off][:, c0 // 16:(c0 + n) // 16], n, [TAB[d], off],
+               ["xg%d_%d" % (d, h) for h in halves])
+
+    def error_sums(src, c0, h, stop, rd):
+        for r in range(4):
+            mm(T["qe%d" % h][:, r:128:4], src[:, c0 + C0[h] + r:c0 + C0[h] + 512:4], T.g1[:], False, stop and r == 3,
+               rd + ["g1"], "qe%d" % h, "qe%d" % h, 64)
+
+    def sums(order):
+        for h in range(2):
+            for d in order:
+                for k, s in enumerate(ORDER[h]):
+                    c0, c1 = 128 * (ND * s + d), 1024 * d + C0[h] + 128 * k
+                    mm(T["qh%d" % h][:, 128 * k:128 * k + 128], T.dg[:, c0:c0 + 128], T.xg[:, c1:c1 + 128], d == order[0] and k == 0,
+                       d == order[-1] and k == 3, ["dg%d_%d" % (s, d), "xg%d_%d" % (d, h)], "qh%d" % h, "qh%d" % h)
+            mm(T["qe%d" % h][:, 0:128], T.ma[0:4, :], T.mb[0:4, :], True, False, ["ma", "mb"], "qe%d" % h, "qe%d" % h)
+            error_sums(T.xg, 5120, h, False, ["xg5_%d" % h])
+
+    def product(a, h):
+        r0, qh, qe = VR * a + 128 * (N - 1) + C0[h], "qh%d" % h, "qe%d" % h
+        tt(T.prod[:, C0[h]:C0[h] + 512], T[qh][:], T.vr[:, r0:r0 + 512], A.mult,
+           [qh, "ret%d_%d" % (a, h)] + ["vg%d_1" % a] * h, ["pr%d" % h], [qh], 512)
+        error_sums(T.prod, 0, h, True, ["pr%d" % h])
+        ac(T.ea[:, 128 * h:128 * h + 128], T[qe][:, 0:128], AF.Abs, 0.0, 0.0625, [qe], ["ea%d" % h], [qe])
 
     def digits(h):
         c = slice(128 * h, 128 * h + 128)
-        ts(T.eb[0:32, c], T.ea[0:32, c], 127.53125, A.add, 191.0, A.min, ["ea%d" % h], ["eb%d" % h])
-        ts(T.ec[0:32, c], T.eb[0:32, c], 129.0, A.max, -160.0, A.add, ["eb%d" % h], ["ec%d" % h])
-        mm(T.qa[:, c], T.pk[0:32, c], T.ec[0:32, c], True, True, ["pk%d" % h, "ec%d" % h], ["qa%d" % h], ["qa"])
+        ts(T.eb[:, c], T.ea[:, c], 127.53125, A.add, 191.0, A.min, ["ea%d" % h], ["eb%d" % h])
+        ts(T.ec[:, c], T.eb[:, c], 129.0, A.max, col(2), A.add, ["eb%d" % h, "col2"], ["ec%d" % h], c=64)
+        mm(T.qa[:, c], T.pk[:], T.ec[:, c], True, True, ["pk", "ec%d" % h], "qa%d" % h, "qa")
 
     def finish(a):
-        sizes(0)
+        product(a, 0), product(a, 1)
         digits(0)
-        errors(a, 1)
-        tt(T.ta[:], T.qa[:, 0:128], T.sa[:], A.mult, ["qa0", "sa"], ["ta"], ["qa"])
-        sizes(1)
-        tt(tv, T.ta[:], cst, A.add, ["ta", "cst"], ["tv"], ["qv"])
+        tt(T.ta[:], T.qa[:, 0:128], T.sab[:, 0:128], A.mult, ["qa0", "sab"], ["ta"], ["qa"])
         digits(1)
-        tt(T.tb[:], T.qa[:, 128:256], T.sb[:], A.mult, ["qa1", "sb"], ["tb"], ["qa"])
+        tt(tv, T.ta[:], cst, A.add, ["ta", "cst"], ["tv"], ["qv", "qa"])
+        tt(T.tb[:], T.qa[:, 128:256], T.sab[:, 128:256], A.mult, ["qa1", "sab"], ["tb"], ["qa"])
         tt(T.ri[:], T.tb[:], tv, A.add, ["tb", "tv"], ["ri"], ["qv"])
         ts(T.pi[:], T.ri[:], 63, A.bitwise_and, None, None, ["ri"], ["pi"])
         cp(P, T.pi[:], ["pi"], ["pp"])
 
-    forward(0, "v")
-    for h in range(2):
-        send("wa%d" % h, h, -1, lambda s: T.dg[:, 640 * OWN:640 * OWN + 640], lambda s: T.dg[:, 640 * s:640 * s + 640],
-             ["dgo%d" % d for d in range(5)], "dg%d" % h)
-    ts(T.npb[:], T.npi[:], 7, A.arith_shift_right, None, None, ["nxi", "pvi"], ["npb"])
-    ts(T.qa[:, 256:512], T.npb[:], -2047.0 / 16.0, A.mult, None, None, ["npb"], ["qa2"], ["qa"])
-    tt(T.npf[:], T.npi[:], T.qa[:, 256:512], A.add, ["nxi", "pvi", "qa2"], ["npf"], ["qa"])
-    ts(T.ppu[:], T.npf[:], 16.0, A.mult, None, None, ["npf"], ["ppu"])
-    open_sums()
-    scales_1()
-    gather("a", T.x2[:], T.x1[:, 0:F], T.ppu[:, 0:128], ["x1", "ppu"], ["x2"])
-    for i in range(16):
-        cp(T.b0p[:, i:F:16], T.b0[:, 128 * i:128 * i + 128], ["b0h", "b0l"], ["b0p%d" % i])
-    b0p = ["b0p%d" % i for i in range(16)]
-    tt(T.a1[:], T.b0[:, 0:F].indirect(T.npu[:, 0:128]), T.b0p[:], A.add, ["b0h", "b0l", "nxu"] + b0p, ["a1"])
-    scales_2()
-    gather("a", T.xm2[:], T.xm1[:, 0:F], T.ppu[:, 128:256], ["xm1", "ppu"], ["xm2"])
-    serve(0, "v", 0)
-    serve(0, "v", 1)
-    tt(T.rwt[:], T.a1[:, 0:F].indirect(T.ppu[:, 0:128]), T.b0p[:], A.add, ["a1", "ppu"] + b0p, ["rwt"])
-    scales_3()
-    pick("a", 2, 0), pick("a", 3, 0), pick("a", 1, 0), pick("a", 4, 0)
-    pick("v", 5, 0), pick("a", 0, 0, True)
-    pick("v", 5, 1), pick("a", 2, 1)
-    errors(0, 0)
-    pick("a", 3, 1), pick("v", 1, 1), pick("a", 4, 1), pick("v", 0, 1, True)
+    for name, out, src, way in (("nx", T.npi[:, 0:128], T.nxt, 400), ("pri", T.prii[:], T.pri, 800), ("x", T.xs[:], T.x, 2000),
+                                ("rw", T.rwi[:], T.rw, 2300), ("key", T.keyi[:], T.key, 2600), ("pv", T.npi[:, 128:256], T.prv, 2900),
+                                ("w", T.ws[:, 0:5], T.w, 3100)):
+        dma("s", "l" + name, out, src[:], (), ["xs" if name == "x" else name + "i"], way)
+    dma("s", "lv0", T.vs[:, 0:V // 2], T.val[:, 0:V // 2], (), ["vs0"], 8000)
+
+    fields()
+    masks()
+    ac(T.wex[:, 0:1], ks4, AF.Exp, 3.0 * LN64, -LN64, ["ktf"], ["wex"], c=1600)
+    lin("a", T.idf[:], T.idb[:], 1.0, 0.0, ["idb"], ["idf"])
+    lin("a", col(3), T.wex[:, 0:1], 1.0, 0.0, ["wex"], ["col3"], n=1)
+    cp(T.npu[:, 0:128], T.npi[:, 0:128], ["nxi"], ["npu0"])
+    state()
+    step("x1", "xs", "npu", 0)
+    rewards()
+    keys()
+    cp(T.npu[:, 128:256], T.npi[:, 128:256], ["pvi"], ["npu128"])
+    step("xm1", "xs", "npu", 128)
+    pointers()
+    for i in range(8):
+        select(T.b1[:, i:F:16], T.b0[:, 128 * i:128 * i + 128], [[0, 128]], A.is_equal, 0, 0, 0, ["b0h", "b0l"], ["b1_%d" % i])
+    running(), forward(0, 0)
+    diagonals()
+    matrices(0), matrices(1)
+    step("x2", "x1", "ppu", 0), step("xm2", "xm1", "ppu", 128)
+    ts(col(1), k3, 0.0, A.is_equal, 31.0, A.mult, ["ktf"], ["col1"], c=1)
+    ts(T.pk[:], T.m16[:], ka, A.is_equal, col(3), A.mult, ["m16", "ktf", "col3"], ["pk"], c=64)
+    ts(col(2), col(1), -191.0, A.add, None, None, ["col1"], ["col2"], c=1)
+    for i in range(8, 16):
+        cp(T.b1[:, i:F:16], T.b0[:, 128 * i:128 * i + 128], ["b0h", "b0l"], ["b1_%d" % i], c=64)
+    reward_step("r1", "b0", "npu", ["b0h", "b0l"])
+    reward_step("r3", "r1", "ppu", ["r1"])
+    part(2, "a")
+    serve(0, 0, "a"), serve(0, 1, "a")
+    part(3, "a"), part(4, "v"), part(0, "v"), part(1, "a", (0,)), part(5, "v"), part(1, "a", (1,))
+    scales()
+    sums((2, 4, 3, 0, 1))
     finish(0)
 
     for a in range(1, R):
-        forward(a, "a")
-        open_sums()
-        scales_1()
-        pick("a", 3, 0)
-        scales_2()
-        pick("v", 5, 0)
-        scales_3()
-        pick("a", 2, 0), pick("v", 1, 0)
-        serve(a, "a", 0)
-        serve(a, "v", 1)
-        pick("a", 4, 0), pick("v", 0, 0, True)
-        pick("a", 2, 1), pick("v", 5, 1), pick("a", 3, 1), pick("v", 1, 1)
-        errors(a, 0)
-        pick("a", 4, 1), pick("a", 0, 1, True)
+        running(), forward(a, 3)
+        part(3, "v"), part(2, "a")
+        serve(a, 0, "a")
+        part(1, "v")
+        serve(a, 1, "a")
+        part(4, "v", (0,)), part(0, "a", (0,)), part(5, "v", (0,))
+        part(4, "a", (1,)), part(0, "v", (1,)), part(5, "a", (1,))
+        scales()
+        sums((2, 3, 1, 4, 0))
         finish(a)
 
     for j in range(8):
-        if j < 5:
-            ts(T.gx[:, j:1024:8], P, T.gw[:, 24 + j:25 + j], A.mult, None, None, ["pp", "gmf"], ["sx%d" % j])
+        lin("vvavvavv"[j], T.gx[:, j:1024:8], P, T.gw[:, 24 + j:25 + j], 0.0, ["pp", "gmf", "p0"], ["sx%d" % j], narrow=True)
+    regroup(T.qk[:, 0:128], lambda j: T.gx[:, 128 * j:128 * j + 128], ["sx%d" % j for j in range(8)], "kt", "qk")
+    lin("v", T.yo[:], T.qk[:, 0:128], 1.0, 0.0, ["kt"], ["yo"], ["qk"])
+    dma("s", "sty", T.y[:], T.yo[:], ["yo"], ["y"], 200)
+
+    Q = {"v": v, "a": act, "p": pe, "g": g, "s": g.sync}
+    count = {"cv": 0, "ca": 0, "cp": 0, "cg": 0}
+    known = {e: {} for e in Q}
+    bank, totals, sent = {}, {}, 0
+    for c in deal(calls):
+        e = c["e"]
+        ev = [calls[j]["ev"] for j in c["pre"]] + [x for b in c["ps"] for q, x in bank.get(b, {}).items() if q != e]
+        for sem, n, clock in sorted(ev, key=lambda x: -x[1]):
+            if known[e].get(sem, 0) < n and not (e == "p" and sem == "cp"):
+                Q[e].wait_ge(T.sem[sem], n)
+                known[e][sem] = n
+                for k, m in clock.items():
+                    known[e][k] = max(known[e].get(k, 0), m)
+        made = c["make"]()
+        if c["n"] < 0:
+            sent -= c["n"]
+            c["ev"] = (c["sem"], -c["n"], {})
         else:
-            ac(T.gx[:, j:1024:8], P, AF.Identity, 0.0, T.gw[:, 24 + j:25 + j], ["pp", "gmf"], ["sx%d" % j])
-    for j in range(8):
-        mm(T.qk[:, 0:128], T.em[:, 112 - 16 * j:240 - 16 * j], T.gx[:, 128 * j:128 * j + 128], j == 0, j == 7,
-           ["em"] + ["sx%d" % k for k in range(8)], ["qk1"], ["qk"])
-    cp(T.yo[:], T.qk[:, 0:128], ["qk1"], ["yo"], ["qk"])
-    dma("s", "sty", T.y[:], T.yo[:], ["yo"], ["y"])
-    g.wait_ge(T.sem.snd, sent[0])
+            sem = c["sem"] or "c" + e
+            made.then_inc(T.sem[sem], c["n"])
+            if not c["sem"]:
+                count[sem] += 1
+            c["ev"] = (sem, count.get(sem, c["n"]), dict(known[e]))
+        for b in c["ps"]:
+            bank.setdefault(b, {})[e] = c["ev"]
+        totals[c["ev"][0]] = c["ev"][1]
+    g.wait_ge(T.sem.snd, sent)
     for sem, n in totals.items():
         if sem != "sty" and max(k.get(sem, 0) for k in known.values()) < n:
             g.wait_ge(T.sem[sem], n)

import math
from concourse.bass import DstId, RemoteDMATransfer
from concourse.mybir import AluOpType, ActivationFunctionType

N, F, V, R = 8, 2048, 8192, 3
W = 1 << 20
LN64 = math.log(64.0)
OWN = 4
RQ, VR = 128, 1920
ND = 5
START, ASTART, WAKE, GATHER, LOAD, ISSUE, FLIGHT, FIRST = 60, 100, 60, 1.56, 1300, 750, 1800, 3500

SBUF = {
    "bfloat16": dict(xs=F, vs=V, ws=8, turn=8, wex=2, um=128, lm=128, nl=128, idb=128, i32=128, nid=128,
                     em=240, pk=128, zb=128, ma=128, mb=128, c240=240, dif=128, m16=128, g1=32,
                     dg=N * ND * 128, x1=F, x2=F, xm1=F, xm2=F, b0=F, b1=F, r1=F, r3=F, rtb=256, prb=128,
                     gx=1024, pp=144, vr=VR * R, xg=6 * 1024, uu=128, samp=128, dp=128, sab=256, eb=256, ec=256),
    "float32": dict(ktf=6, j8=8, col=8, idf=128, gw=56, rst=128, keyf=128, sm=128, zz=128, cl=1024, ea=256, yo=128, npf=256),
    "int32": dict(npi=256, npb=256, keyi=128, rwi=128, prii=128, kci=2, kti=6, rti=256, si=128, low=128, t1=128,
                  ki=64, ks=64, pl=64, ta=128, tb=128, ri=128, pi=128),
    "uint16": dict(npu=256, ppu=256, tu=64, tp=64, rq=RQ * R),
    "float16": dict(prod=1024),
}
SCRATCH = {n: ("sbuf", [128, c], d) for d, group in SBUF.items() for n, c in group.items()}
SCRATCH.update({n: ("psum", [128, 512], "float32") for n in ("qd", "qv", "qk", "qa", "qh0", "qh1", "qe0", "qe1")})
SEMAPHORES = (["cv", "ca", "cp", "cg", "snd", "lw", "lpri", "lnx", "lpv", "lkey", "lrw", "lx", "lv0", "lv1", "lb0", "lb1", "lb2", "lb3", "sty"]
              + ["wa%d" % h for h in range(2)]
              + ["rq%d_%d" % (a, h) for a in range(R) for h in range(2)] + ["rt%d_%d" % (a, h) for a in range(R) for h in range(2)])

A = AluOpType
AF = ActivationFunctionType
HALF = ((0, 1, 2, 3), (5, 6, 7))
ORDER = ((3, 2, 1, 0), (4, 5, 6, 7))


def asked(s):
    return s if s < OWN else (N - 1 if s == OWN else s - 1)


def kept(s):
    return N - 1 + (s - OWN if s >= OWN else N - 1 - s)


DEALT = []


def deal(calls):
    wrote, read = {}, {}
    for k, c in enumerate(calls):
        pre = {wrote[r] for r in c["rd"] + c["wr"] if r in wrote}
        for w in c["wr"]:
            pre.update(read.get(w, ()))
        c["pre"] = pre - {k}
        for r in c["rd"]:
            read.setdefault(r, []).append(k)
        for w in c["wr"]:
            wrote[w], read[w] = k, []
    if not DEALT:
        taken, last = {}, {}
        for c in calls:
            e = c["e"]
            t = max([0 if e == "p" else last.get(e, 0)] + [calls[j]["end"] + (0 if calls[j]["e"] == e else WAKE) for j in c["pre"]])
            spans = [x for x in taken.get(e, []) if x[1] > t]
            spans += [(a - WAKE, b + WAKE, q) for bk in c["ps"] for a, b, q in taken.get(bk, []) if q != e and b + WAKE > t]
            for a, b, _ in sorted(spans):
                if a >= t + c["busy"]:
                    break
                t = max(t, b)
            c["start"], c["end"], last[e] = t, t + c["busy"] + c["way"], t + c["busy"]
            for r in (e,) + tuple(c["ps"]):
                taken.setdefault(r, []).append((t, t + c["busy"], e))
        DEALT.extend(sorted(range(len(calls)), key=lambda k: (calls[k]["start"], k)))
    return [calls[k] for k in DEALT]


def rank_program(g, core, T, topo):
    rank = T.rank_of(core)
    if rank is None:
        return
    v, act, pe = g.vector, g.scalar, g.tensor
    calls = []

    def call(e, busy, make, rd, wr, ps=(), way=0, sem=None, n=1):
        calls.append(dict(e=e, busy=busy, make=make, rd=list(rd), wr=list(wr), ps=ps, way=way, sem=sem, n=n))

    def vop(make, rd, wr, ps=(), c=128):
        call("v", START + max(64, c), make, rd, wr, ps)

    def ts(out, in0, s1, op0, s2, op1, rd, wr, ps=(), c=128):
        if op1 is None:
            vop(lambda: v.tensor_scalar(out, in0, s1, None, op0), rd, wr, ps, c)
        else:
            vop(lambda: v.tensor_scalar(out, in0, s1, s2, op0, op1), rd, wr, ps, c)

    def tt(out, in0, in1, o, rd, wr, ps=(), c=128):
        vop(lambda: v.tensor_tensor(out, in0, in1, o), rd, wr, ps, c)

    def cp(out, in_, rd, wr, ps=(), c=128):
        vop(lambda: v.tensor_copy(out, in_), rd, wr, ps, c)

    def ac(out, in_, func, bias, scale, rd, wr, ps=(), c=128):
        call("a", ASTART + c, lambda: act.activation(out, in_, func, bias=bias, scale=scale), rd, wr, ps)

    def lin(on, out, in_, scale, bias, rd, wr, ps=(), n=128, narrow=False):
        if on == "a":
            ac(out, in_, AF.Identity, bias, scale, rd, wr, ps, n)
        else:
            ts(out, in_, scale, A.mult, bias, A.add, rd, wr, ps, n // 2 if narrow else n)

    def gather(on, out, win, off, n, rd, wr):
        if on == "a":
            ac(out, win.indirect(off), AF.Identity, 0.0, 1.0, rd, wr, (), GATHER * n - 120)
        else:
            cp(out, win.indirect(off), rd, wr, (), GATHER * n)

    def mm(out, lhsT, rhs, start, stop, rd, reg, b, c=128):
        ends = start or stop
        call("p", c // 2, lambda: pe.matmul(out, lhsT, rhs, start, stop), rd + ([] if ends else [reg, "open " + b]),
             [reg, "open " + b] if ends else [], (b,))

    def dma(e, sem, out, in_, rd, wr, way):
        call(e, 60, lambda: {"s": g.sync, "a": act}[e].dma_start(out, in_), rd, wr, (), LOAD + way, sem, 16)

    def send(sem, h, step, src, dst, rd, wr, way, first=False):
        def make():
            tr = []
            for j, s in enumerate(HALF[h]):
                to = T.cores[(rank + step * (s + 4)) % N]
                rid, pid, _ = topo.addr(to)
                mask = sum(1 << x for x in topo.engines(core, to)[j::4])
                tr.append(RemoteDMATransfer(dst_ids=[DstId(rid=rid, pnc=pid)], dma_engine_mask=mask,
                                            remote_sem=T.sem[sem], src=src(s), dst=dst(s)))
            g.remote_dma_fused(tr, local_sem=T.sem.snd)
        call("g", ISSUE + FIRST * first, make, rd, wr, (), FLIGHT - ISSUE + way, sem, -4 * len(HALF[h]))

    def iota(out, pattern, base, cm, wr, fl=True):
        n = math.prod(c for _, c in pattern)
        if fl:
            call("g", 160 + 2 * n, lambda: g.iota(out, pattern, base, cm, allow_small_or_imprecise_dtypes=True), (), wr)
        else:
            call("g", 160 + 2 * n, lambda: g.iota(out, pattern, base, cm), (), wr)

    def select(out, in_, pattern, test, fill, base, cm, rd, wr):
        n = math.prod(c for _, c in pattern)
        call("g", 200 + 2 * n, lambda: g.affine_select(out, in_, pattern, test, float(fill), base, cm), rd, wr)

    def band(name, c, test=A.not_equal):
        select(T[name][:], T.zb[:], [[1, 128]], test, c, 0, -1, ["zb"], [name])

    def group_mask(out, zeros, pattern, c, rd, wr):
        select(out, zeros, pattern, A.is_gt, c, 0, -1, rd, wr)
        select(out, out, pattern, A.is_ge, 0, 15, -1, [], wr)

    def col(j):
        return T.col[:, j:j + 1]

    P = T.pp[:, 16:144]
    gmf = T.gw[:, 24:32]
    kmod, ka, ks4, k3, k128, kdiv = (T.ktf[:, k:k + 1] for k in range(6))
    z1, tv = T.qv[:, 128:256], T.qv[:, 256:384]
    pq, cst = T.qa[:, 256:384], T.qa[:, 384:512]
    C0 = (512, 0)
    TAB = ["xm2", "xm1", "xs", "x1", "x2", "r3"]

    def fields():
        iota(T.kci[:, 0:1], [[1, 1]], 0, 1, ["kc0"], False)
        iota(T.dif[:], [[1, 128]], 0, -1, ["dif"])
        iota(T.kci[:, 1:2], [[1, 1]], 0, 128, ["kc1"], False)
        iota(T.j8[:], [[1, 8]], 0, 0, ["j8"])
        iota(T.c240[:], [[1, 240]], -112, 0, ["c240"])
        for ap, x, reg in ((T.zb[:], 0.0, "zb"), (T.gw[:], 0.0, "gw"), (T.rst[:], 1.0, "rst")):
            vop(lambda ap=ap, x=x: v.memset(ap, x), (), [reg], c=64)
        vop(lambda: v.memset(T.b0[:, 0:1024], 0.0), (), ["b0z"], c=512)
        for j, c, shift, mask in ((2, 0, 5, 3), (5, 0, 4, 7), (0, 0, 0, 15), (1, 0, 2, 7), (3, 0, 0, 3), (4, 1, 0, 15 * 128)):
            ts(T.kti[:, j:j + 1], T.kci[:, c:c + 1], shift, A.arith_shift_right, mask, A.bitwise_and, ["kc%d" % c], ["kt%d" % j], c=1)
        cp(T.ktf[:], T.kti[:], ["kt%d" % k for k in range(6)], ["ktf"], c=6)
        ts(T.idb[:], T.dif[:], 0.0, A.is_equal, None, None, ["dif"], ["idb"], c=64)
        ts(gmf, T.j8[:], kdiv, A.is_equal, None, None, ["j8", "ktf", "gw"], ["gmf"], c=8)
        vop(lambda: v.memset(T.b0[:, 1024:F], 0.0), ["b0z"], ["b0h", "b0l"], c=512)
        ts(T.em[:], T.c240[:], kmod, A.is_equal, None, None, ["c240", "ktf"], ["em"])
        vop(lambda: v.memset(T.rst[:, 0:128:16], 0.0), (), ["rst"], c=8)

    def masks():
        select(T.um[:], T.zb[:], [[-1, 128]], A.is_gt, 8192, 0, 1, ["zb"], ["um"])
        band("lm", 8192.0, A.is_ge), band("nl", -8192.0, A.is_ge), band("i32", 32.0)
        iota(T.turn[:], [[0, 8]], (-rank - 5) % N * W // 32, 0, ["turn"])
        iota(col(0), [[1, 1]], -4 * W, 1, ["col0"])
        iota(T.pp[:, 0:16], [[0, 16]], 0, 0, ["pad"])
        group_mask(T.gw[:, 16:24], T.gw[:, 16:24], [[16, 8]], -1, ["gw"], ["gmn"])
        iota(T.m16[:], [[1, 8], [0, 16]], 0, 0, ["m16"])
        band("nid", -1.0)
        select(T.ma[0:4, :], T.zb[0:4, :], [[0, 32], [1, 4]], A.not_equal, 1, 0, -1, ["zb"], ["ma"])
        select(T.mb[0:4, :], T.zb[0:4, :], [[0, 8], [1, 4], [0, 4]], A.is_equal, 32768, 0, -1, ["zb"], ["mb"])
        group_mask(T.g1[:], T.zb[:, 0:32], [[16, 8], [0, 4]], 1, ["zb"], ["g1"])

    def diagonals():
        for d in range(ND):
            c0 = 128 * (ND * OWN + d)
            lin("v", T.dg[:, c0:c0 + 128], T.idb[:], T.ws[:, d:d + 1], 0.0, ["idb", "wi"], ["dg%d_%d" % (OWN, d)], narrow=True)

    def matrices(h):
        send("wa%d" % h, h, -1, lambda s: T.dg[:, 128 * ND * OWN:128 * ND * (OWN + 1)], lambda s: T.dg[:, 128 * ND * s:128 * ND * (s + 1)],
             ["dg%d_%d" % (OWN, d) for d in range(ND)], ["dg%d_%d" % (s, d) for s in HALF[h] for d in range(ND)], 1000)

    def rewards():
        ts(T.rti[:, 0:128], T.rwi[:], -32, A.bitwise_and, None, None, ["rwi"], ["rt0"])
        ts(T.rti[:, 128:256], T.rwi[:], 31, A.bitwise_and, None, None, ["rwi"], ["rt1"])
        cp(T.rtb[:], T.rti[:], ["rt0", "rt1"], ["rtb"], c=256)
        dma("s", "lb0", T.b0[0:128:16, :], T.rtb[:, 0:128], ["rtb"], ["b0h"], 1200)
        dma("s", "lb1", T.b0[1:128:16, :], T.rtb[:, 128:256], ["rtb"], ["b0l"], 1500)
        dma("s", "lv1", T.vs[:, V // 2:V], T.val[:, V // 2:V], (), ["vs1"], 6000)

    def regroup(out, src, rd, reg, b):
        for j in range(8):
            mm(out, T.em[:, 112 - 16 * j:240 - 16 * j], src(j), j == 0, j == 7, ["em"] + rd, reg, b)

    def pointers():
        ts(T.npb[:], T.npi[:], 7, A.arith_shift_right, None, None, ["nxi", "pvi"], ["npb"], c=256)
        ts(T.qh0[:, 0:256], T.npb[:], -2047.0 / 16.0, A.mult, None, None, ["npb"], ["qh0"], ["qh0"], 256)
        tt(T.npf[:], T.npi[:], T.qh0[:, 0:256], A.add, ["nxi", "pvi", "qh0"], ["npf"], ["qh0"], 256)
        ts(T.ppu[:], T.npf[:], 16.0, A.mult, None, None, ["npf"], ["ppu0", "ppu128"], c=256)

    def state():
        cp(T.prb[:], T.prii[:], ["prii"], ["prb"])
        for j in range(8):
            lin("v", T.gx[:, 128 * j:128 * j + 128], T.prb[:], T.gw[:, 24 + j:25 + j], 0.0, ["prb", "gmf"], ["gx%d" % j], narrow=True)
        regroup(T.qd[:, 128:256], lambda j: T.gx[:, j:1024:8], ["gx%d" % j for j in range(8)], "p0", "qd")

    def keys():
        cp(T.keyf[:], T.keyi[:], ["keyi"], ["keyf"])
        mm(T.qk[:, 0:128], T.keyf[:], T.idf[:], True, True, ["keyf", "idf"], "kt", "qk", 512)
        lin("v", P, T.qd[:, 128:256], 1.0, 0.0, ["p0"], ["pp"], ["qd"])
        lin("v", T.qv[:, 0:128], T.qk[:, 0:128], 128.0, col(0), ["kt", "col0"], ["base"], ["qk", "qv"])

    def step(name, src, off, c0):
        gather("a", T[name][:], T[src][:, 0:F], T[off][:, c0:c0 + 128], F, [src, off + str(c0)], [name])

    def reward_step(name, src, off, rd):
        tt(T[name][:], T[src][:, 0:F].indirect(T[off][:, 0:128]), T.b1[:], A.add, rd + ["b1_%d" % i for i in range(16)] + [off + "0"],
           [name], c=GATHER * F)

    def running():
        mm(T.qd[:, 0:128], T.um[:], P, True, False, ["um", "pp"], "dd", "qd")
        mm(T.qd[:, 0:128:16], T.i32[:], T.turn[:], False, False, ["i32", "turn"], "dd", "qd", 64)
        mm(T.qd[:, 0:128], T.lm[:], T.pp[:, 15:143], False, False, ["lm", "pp", "pad"], "dd", "qd")
        mm(T.qd[:, 16:128:16], T.nl[:], T.pp[:, 31:143:16], False, True, ["nl", "pp"], "dd", "qd", 64)
        mm(pq, T.idb[:], P, True, True, ["idb", "pp"], "pq", "qa")

    def forward(a, on_scalar):
        vop(lambda: v.tensor_tensor_scan(T.si[:], T.rst[:], T.qd[:, 0:128], 0.0, A.mult, A.add), ["rst", "dd"], ["si"], ["qd"])
        ts(T.low[:], T.si[:], 13, A.arith_shift_right, 127, A.bitwise_and, ["si"], ["low"])
        ts(T.t1[:], T.si[:], 7 << 20, A.bitwise_and, None, None, ["si"], ["t1"])
        tt(T.samp[:], T.low[:], pq, A.is_lt, ["low", "pq"], ["samp"], ["qa"])
        tt(z1, T.t1[:], T.qv[:, 0:128], A.add, ["t1", "base"], ["z1"], ["qv"])
        tt(T.zz[:], z1, T.samp[:], A.mult, ["z1", "samp"], ["zz"], ["qv"])
        cl = lambda h, j: T.cl[:, 512 * h + 128 * j:512 * h + 128 * j + 128]
        todo = [(0, 0), (1, 0), (0, 1), (0, 2), (1, 1), (0, 3), (1, 2), (1, 3)]
        for h, j in todo:
            if h == 0:
                ts(cl(h, j), T.zz[:], float(j * W), A.add, 0.0, A.min, ["zz"], ["cl%d_%d" % (h, j)])
            elif j < on_scalar:
                ac(cl(h, j), T.zz[:], AF.Relu, -float(j * W), 1.0, ["zz"], ["cl%d_%d" % (h, j)])
            else:
                ts(cl(h, j), T.zz[:], -float(j * W), A.add, 0.0, A.max, ["zz"], ["cl%d_%d" % (h, j)])
        for h, j in todo:
            c0 = 256 + C0[h] // 16
            mm(T.qd[:, c0:c0 + 32], cl(h, j), T.gw[:, 24 - 8 * j:56 - 8 * j], (h, j) == todo[0], (h, j) == todo[-1],
               ["cl%d_%d" % (h, j), "gmf", "gmn"], "pick", "qd", 256)
        ts(T.uu[:], T.t1[:], 1.0 / (8 * W), A.mult, -3.5 / 8, A.add, ["t1"], ["uu"])
        kept_priorities()
        cp(T.ki[:], T.qd[:, 256:320], ["pick"], ["ki"], ["qd"], 64)
        ts(T.ks[:], T.ki[:], 7, A.arith_shift_right, V - 1, A.bitwise_and, ["ki"], ["ks"], c=64)
        ts(T.pl[:], T.ki[:], 127, A.bitwise_and, None, None, ["ki"], ["pl"], c=64)
        cp(T.rq[:, RQ * a + 56:RQ * a + 120], T.ks[:], ["ks"], ["ku%d" % a], c=64)
        for h in range(2):
            send("rq%d_%d" % (a, h), h, 1, lambda s: T.rq[:, RQ * a + 8 * kept(s):RQ * a + 8 * kept(s) + 8],
                 lambda s: T.rq[:, RQ * a + 8 * asked(s):RQ * a + 8 * asked(s) + 8], ["ku%d" % a], ["req%d_%d" % (a, h)], 0, a == h == 0)
        ts(T.tp[:], T.pl[:], 16.0, A.mult, kmod, A.add, ["pl", "ktf"], ["tp"], c=64)
        ts(T.tu[:], T.pl[:], k128, A.add, None, None, ["pl", "ktf"], ["tu"], c=64)

    def scales():
        for k, m in enumerate(("idb", "nid")):
            out = T.qk[:, 128 + 128 * k:256 + 128 * k]
            mm(out, T[m][:], T.uu[:], True, False, [m, "uu"], "y%d" % k, "qk")
            mm(out, T.nid[:], T.samp[:], False, True, ["nid", "samp"], "y%d" % k, "qk")
        ac(T.sab[:], T.qk[:, 128:384], AF.Exp, -11.5 * LN64, -8.0 * LN64, ["y0", "y1"], ["sab"], ["qk"], 256)

    def kept_priorities():
        tt(T.dp[:], T.samp[:], pq, A.mult, ["samp", "pq"], ["dp"], ["qa"])
        mm(cst, T.idb[:], P, True, False, ["idb", "pp"], "cst", "qa")
        mm(cst, T.i32[:], T.samp[:], False, False, ["i32", "samp"], "cst", "qa")
        mm(cst, T.nid[:], T.dp[:], False, True, ["nid", "dp"], "cst", "qa")

    def serve(a, h, on):
        c0 = VR * a + 512 * h
        gather(on, T.vr[:, c0:c0 + 512], T.vs[:, 0:V], T.rq[:, RQ * a + 32 * h:RQ * a + 32 * h + 32], 512,
               ["vs0", "vs1", "req%d_%d" % (a, h)] + ["ku%d" % a] * h, ["vg%d_%d" % (a, h)])
        send("rt%d_%d" % (a, h), h, -1, lambda s: T.vr[:, VR * a + 128 * asked(s):VR * a + 128 * asked(s) + 128],
             lambda s: T.vr[:, VR * a + 128 * kept(s):VR * a + 128 * kept(s) + 128], ["vg%d_%d" % (a, h)], ["ret%d_%d" % (a, h)], 400)

    def part(d, on, halves=(0, 1)):
        c0, n, off = min(C0[h] for h in halves), 512 * len(halves), "tu" if d == 2 else "tp"
        gather(on, T.xg[:, 1024 * d + c0:1024 * d + c0 + n], T[TAB[d]][:, 0:F], T[off][:, c0 // 16:(c0 + n) // 16], n, [TAB[d], off],
               ["xg%d_%d" % (d, h) for h in halves])

    def error_sums(src, c0, h, stop, rd):
        for r in range(4):
            mm(T["qe%d" % h][:, r:128:4], src[:, c0 + C0[h] + r:c0 + C0[h] + 512:4], T.g1[:], False, stop and r == 3,
               rd + ["g1"], "qe%d" % h, "qe%d" % h, 64)

    def sums(order):
        for h in range(2):
            for d in order:
                for k, s in enumerate(ORDER[h]):
                    c0, c1 = 128 * (ND * s + d), 1024 * d + C0[h] + 128 * k
                    mm(T["qh%d" % h][:, 128 * k:128 * k + 128], T.dg[:, c0:c0 + 128], T.xg[:, c1:c1 + 128], d == order[0] and k == 0,
                       d == order[-1] and k == 3, ["dg%d_%d" % (s, d), "xg%d_%d" % (d, h)], "qh%d" % h, "qh%d" % h)
            mm(T["qe%d" % h][:, 0:128], T.ma[0:4, :], T.mb[0:4, :], True, False, ["ma", "mb"], "qe%d" % h, "qe%d" % h)
            error_sums(T.xg, 5120, h, False, ["xg5_%d" % h])

    def product(a, h):
        r0, qh, qe = VR * a + 128 * (N - 1) + C0[h], "qh%d" % h, "qe%d" % h
        tt(T.prod[:, C0[h]:C0[h] + 512], T[qh][:], T.vr[:, r0:r0 + 512], A.mult,
           [qh, "ret%d_%d" % (a, h)] + ["vg%d_1" % a] * h, ["pr%d" % h], [qh], 512)
        error_sums(T.prod, 0, h, True, ["pr%d" % h])
        ac(T.ea[:, 128 * h:128 * h + 128], T[qe][:, 0:128], AF.Abs, 0.0, 0.0625, [qe], ["ea%d" % h], [qe])

    def digits(h):
        c = slice(128 * h, 128 * h + 128)
        ts(T.eb[:, c], T.ea[:, c], 127.53125, A.add, 191.0, A.min, ["ea%d" % h], ["eb%d" % h])
        ts(T.ec[:, c], T.eb[:, c], 129.0, A.max, col(2), A.add, ["eb%d" % h, "col2"], ["ec%d" % h], c=64)
        mm(T.qa[:, c], T.pk[:], T.ec[:, c], True, True, ["pk", "ec%d" % h], "qa%d" % h, "qa")

    def finish(a):
        product(a, 0), product(a, 1)
        digits(0)
        tt(T.ta[:], T.qa[:, 0:128], T.sab[:, 0:128], A.mult, ["qa0", "sab"], ["ta"], ["qa"])
        digits(1)
        tt(tv, T.ta[:], cst, A.add, ["ta", "cst"], ["tv"], ["qv", "qa"])
        tt(T.tb[:], T.qa[:, 128:256], T.sab[:, 128:256], A.mult, ["qa1", "sab"], ["tb"], ["qa"])
        tt(T.ri[:], T.tb[:], tv, A.add, ["tb", "tv"], ["ri"], ["qv"])
        ts(T.pi[:], T.ri[:], 63, A.bitwise_and, None, None, ["ri"], ["pi"])
        cp(P, T.pi[:], ["pi"], ["pp"])

    for name, out, src, way in (("nx", T.npi[:, 0:128], T.nxt, 400), ("pri", T.prii[:], T.pri, 800), ("x", T.xs[:], T.x, 2000),
                                ("rw", T.rwi[:], T.rw, 2300), ("key", T.keyi[:], T.key, 2600), ("pv", T.npi[:, 128:256], T.prv, 2900),
                                ("w", T.ws[:, 0:5], T.w, 3100)):
        dma("s", "l" + name, out, src[:], (), ["xs" if name == "x" else name + "i"], way)
    dma("s", "lv0", T.vs[:, 0:V // 2], T.val[:, 0:V // 2], (), ["vs0"], 8000)

    fields()
    masks()
    ac(T.wex[:, 0:1], ks4, AF.Exp, 3.0 * LN64, -LN64, ["ktf"], ["wex"], c=1600)
    lin("a", T.idf[:], T.idb[:], 1.0, 0.0, ["idb"], ["idf"])
    lin("a", col(3), T.wex[:, 0:1], 1.0, 0.0, ["wex"], ["col3"], n=1)
    cp(T.npu[:, 0:128], T.npi[:, 0:128], ["nxi"], ["npu0"])
    state()
    step("x1", "xs", "npu", 0)
    rewards()
    keys()
    cp(T.npu[:, 128:256], T.npi[:, 128:256], ["pvi"], ["npu128"])
    step("xm1", "xs", "npu", 128)
    pointers()
    for i in range(8):
        select(T.b1[:, i:F:16], T.b0[:, 128 * i:128 * i + 128], [[0, 128]], A.is_equal, 0, 0, 0, ["b0h", "b0l"], ["b1_%d" % i])
    running(), forward(0, 0)
    diagonals()
    matrices(0), matrices(1)
    step("x2", "x1", "ppu", 0), step("xm2", "xm1", "ppu", 128)
    ts(col(1), k3, 0.0, A.is_equal, 31.0, A.mult, ["ktf"], ["col1"], c=1)
    ts(T.pk[:], T.m16[:], ka, A.is_equal, col(3), A.mult, ["m16", "ktf", "col3"], ["pk"], c=64)
    ts(col(2), col(1), -191.0, A.add, None, None, ["col1"], ["col2"], c=1)
    for i in range(8, 16):
        cp(T.b1[:, i:F:16], T.b0[:, 128 * i:128 * i + 128], ["b0h", "b0l"], ["b1_%d" % i], c=64)
    reward_step("r1", "b0", "npu", ["b0h", "b0l"])
    reward_step("r3", "r1", "ppu", ["r1"])
    part(2, "a")
    serve(0, 0, "a"), serve(0, 1, "a")
    part(3, "a"), part(4, "v"), part(0, "v"), part(1, "a", (0,)), part(5, "v"), part(1, "a", (1,))
    scales()
    sums((2, 4, 3, 0, 1))
    finish(0)

    for a in range(1, R):
        running(), forward(a, 3)
        part(3, "v"), part(2, "a")
        serve(a, 0, "a")
        part(1, "v")
        serve(a, 1, "a")
        part(4, "v", (0,)), part(0, "a", (0,)), part(5, "v", (0,))
        part(4, "a", (1,)), part(0, "v", (1,)), part(5, "a", (1,))
        scales()
        sums((2, 3, 1, 4, 0))
        finish(a)

    for j in range(8):
        lin("vvavvavv"[j], T.gx[:, j:1024:8], P, T.gw[:, 24 + j:25 + j], 0.0, ["pp", "gmf", "p0"], ["sx%d" % j], narrow=True)
    regroup(T.qk[:, 0:128], lambda j: T.gx[:, 128 * j:128 * j + 128], ["sx%d" % j for j in range(8)], "kt", "qk")
    lin("v", T.yo[:], T.qk[:, 0:128], 1.0, 0.0, ["kt"], ["yo"], ["qk"])
    dma("s", "sty", T.y[:], T.yo[:], ["yo"], ["y"], 200)

    Q = {"v": v, "a": act, "p": pe, "g": g, "s": g.sync}
    count = {"cv": 0, "ca": 0, "cp": 0, "cg": 0}
    known = {e: {} for e in Q}
    bank, totals, sent = {}, {}, 0
    for c in deal(calls):
        e = c["e"]
        ev = [calls[j]["ev"] for j in c["pre"]] + [x for b in c["ps"] for q, x in bank.get(b, {}).items() if q != e]
        for sem, n, clock in sorted(ev, key=lambda x: -x[1]):
            if known[e].get(sem, 0) < n and not (e == "p" and sem == "cp"):
                Q[e].wait_ge(T.sem[sem], n)
                known[e][sem] = n
                for k, m in clock.items():
                    known[e][k] = max(known[e].get(k, 0), m)
        made = c["make"]()
        if c["n"] < 0:
            sent -= c["n"]
            c["ev"] = (c["sem"], -c["n"], {})
        else:
            sem = c["sem"] or "c" + e
            made.then_inc(T.sem[sem], c["n"])
            if not c["sem"]:
                count[sem] += 1
            c["ev"] = (sem, count.get(sem, c["n"]), dict(known[e]))
        for b in c["ps"]:
            bank.setdefault(b, {})[e] = c["ev"]
        totals[c["ev"][0]] = c["ev"][1]
    g.wait_ge(T.sem.snd, sent)
    for sem, n in totals.items():
        if sem != "sty" and max(k.get(sem, 0) for k in known.values()) < n:
            g.wait_ge(T.sem[sem], n)
    g.sync.wait_ge(T.sem.sty, 16)
